import numpy as np
import ml_dtypes


def mxq(x, axis, fmt="e4m3"):
    dtype, down = {"e4m3": (ml_dtypes.float8_e4m3fn, 7), "e5m2": (ml_dtypes.float8_e5m2, 14)}[fmt]
    v = np.moveaxis(np.asarray(x, np.float32).astype(ml_dtypes.bfloat16).astype(np.float64), axis, -1)
    blocks = v.reshape(v.shape[:-1] + (-1, 32))
    amax = np.abs(blocks).max(-1, keepdims=True)
    byte = np.maximum(np.where(amax > 0, np.frexp(amax)[1] - 1 + 127, 0) - down, 1)
    scale = np.exp2(byte - 127.0)
    codes = (blocks / scale).astype(np.float32).astype(dtype).astype(np.float64)
    return np.moveaxis((codes * scale).reshape(v.shape), -1, axis)


WIDE = False


def mx_kscale(k):
    if not WIDE:
        return np.ones(k)
    levels = np.array([10, -10, 5, -5, 0])
    if k % 512:
        return np.exp2(np.random.permutation(np.resize(levels, k // 32))).repeat(32)
    a = np.empty((k // 512, 16))
    for p in range(k // 512):
        a[p, :8] = np.random.permutation(np.resize(levels, 8))
        for g in range(8):
            far = levels[np.abs(levels - a[p, g]) >= 10]
            a[p, g + 8] = far[np.random.randint(len(far))]
    return np.exp2(a.ravel()).repeat(32)


def f64(x):
    return np.asarray(x).astype(np.float64)


def striped(idx):
    return np.tile(idx.reshape(-1, 16).T, (8, 1)).astype(np.uint16)


def unstriped(offs):
    return offs[:16].T.reshape(-1).astype(np.int64)


def pack_weight(w):
    k, n = w.shape
    w = f64(np.asarray(w, np.float32).astype(ml_dtypes.bfloat16)).reshape(k // 32, 32, n)
    amax = np.abs(w).max(1)
    byte = np.clip(np.where(amax > 0, np.frexp(amax)[1] - 1 + 127 - 7, 1), 1, 254)
    scaled = (w * np.exp2(127.0 - byte)[:, None, :]).reshape(k, n).astype(np.float32)
    words = np.ascontiguousarray(scaled.reshape(k // 512, 128, 4, n).transpose(0, 1, 3, 2)).astype(ml_dtypes.float8_e4m3fn).view(np.uint8)
    return words, np.ascontiguousarray(byte.astype(np.uint8).reshape(k // 512, 16, n))


def unpack_weight(words, scales):
    g, p, n, _ = words.shape
    vals = np.ascontiguousarray(words).view(ml_dtypes.float8_e4m3fn).astype(np.float64) * np.repeat(np.exp2(scales.astype(np.float64) - 127.0), 8, axis=1)[..., None]
    return vals.transpose(0, 1, 3, 2).reshape(g * 512, n)


def relu(v):
    return np.maximum(v, 0.0)


K, T, S, H, N, U = 1024, 2048, 1024, 512, 256, 2048
P = 2 ** 7


def setup_inputs():
    n = np.random.standard_normal
    s = mx_kscale(K)[:, None]
    u = mx_kscale(H)
    packed_xT = pack_weight(n((K, T)) * s)
    packed_w2 = pack_weight(n((H, N)) / np.sqrt(H) / u[:, None])
    return {
        "x_words": packed_xT[0],
        "x_scales": packed_xT[1],
        "gate": np.tile(np.random.uniform(0.5, 1.5, S), (P, 1)).astype(np.float32),
        "w1": (n((K, H)) / np.sqrt(K) / s * u).astype(np.float32),
        "w2_words": packed_w2[0],
        "w2_scales": packed_w2[1],
        "offs": striped(np.random.permutation(T)[:S]),
        "dst": striped(np.random.permutation(U)[:S]),
    }


def reference(x_words, x_scales, gate, w1, w2_words, w2_scales, offs, dst):
    xq = unpack_weight(x_words, x_scales)[:, unstriped(offs)]
    h = relu(mxq(f64(w1), 0, "e4m3").T @ xq)
    y = unpack_weight(w2_words, w2_scales).T @ mxq(h, 0, "e4m3")
    out = np.zeros((N, U))
    out[:, unstriped(dst)] = y * f64(gate)[:1]
    return out

@@ -1,0 +1,202 @@
+from contextlib import ExitStack
+
+import concourse.mybir as mybir
+
+K, T, S, H, N, U = 1024, 2048, 1024, 512, 256, 2048
+FLOPS = 2 * K * H * S + 2 * H * N * S
+
+F32 = mybir.dt.float32
+BF16 = mybir.dt.bfloat16
+I32 = mybir.dt.int32
+U32 = mybir.dt.uint32
+U16 = mybir.dt.uint16
+U8 = mybir.dt.uint8
+FP8X4 = mybir.dt.float8_e4m3fn_x4
+RELU = mybir.ActivationFunctionType.Relu
+MULT = mybir.AluOpType.mult
+
+P = 128
+PACK = 4
+PASSES = K // (P * PACK)
+TILE = 128
+CHUNK = 256
+LANES = 16
+
+
+def tile_picked_route2_mlprelu_p_kernel(tc, x_words, x_scales, gate, w1, w2_words, w2_scales, offs, dst, out):
+    nc = tc.nc
+    with ExitStack() as ctx:
+        keep = ctx.enter_context(tc.tile_pool(name="keep", bufs=1))
+        psum = ctx.enter_context(tc.psum_pool(name="psum", bufs=1))
+
+        offs_sb = keep.tile([P, S // LANES], U16, name="offs_sb")
+        dst_sb = keep.tile([P, S // LANES], U16, name="dst_sb")
+        x_win = [keep.tile([P, T], I32, name="x_win%d" % g, align_bytes=64) for g in range(PASSES)]
+        xs_win = keep.tile([P, T], U8, name="xs_win", align_bytes=64)
+        x_pick = [keep.tile([P, S], U32, name="x_pick%d" % g, align_bytes=64) for g in range(PASSES)]
+        xs_pick = keep.tile([P, S], U8, name="xs_pick", align_bytes=64)
+        w1_raw = [
+            keep.tile([P, PACK, H], F32, name="w1_raw%d" % g, tag="stage%d" % g, align_bytes=64)
+            for g in range(PASSES)
+        ]
+        xs_rows = keep.tile([P, T // 4], I32, name="xs_rows", align_bytes=64)
+        w1_bf = [keep.tile([P, PACK * H], BF16, name="w1_bf%d" % g, align_bytes=64) for g in range(PASSES)]
+        w1_codes = [keep.tile([P, H], U32, name="w1_codes%d" % g, align_bytes=64) for g in range(PASSES)]
+        w1_sc = [keep.tile([P, H], U8, name="w1_sc%d" % g, align_bytes=64) for g in range(PASSES)]
+        w2_codes = keep.tile([P, N], I32, name="w2_codes", align_bytes=64)
+        w2_sc = keep.tile([P, N], U8, name="w2_sc", align_bytes=64)
+        gate_sb = keep.tile([P, S], F32, name="gate_sb", align_bytes=64)
+        h_bf = keep.tile([P, PACK * S], BF16, name="h_bf", align_bytes=64)
+        h_codes = keep.tile([P, S], U32, name="h_codes", align_bytes=64)
+        h_sc = keep.tile([P, S], U8, name="h_sc", align_bytes=64)
+        y_sb = [keep.tile([P, S], F32, name="y_sb%d" % b, align_bytes=64) for b in range(N // P)]
+        placed = [keep.tile([P, U], F32, name="placed0", align_bytes=64)]
+        zero = keep.tile([P, 1], F32, name="zero")
+        banks = [psum.tile([P, PACK * TILE], F32, name="bank%d" % i) for i in range(S // TILE)]
+
+        nc.vector.memset(xs_win[:].bitcast(I32), 0)
+        nc.vector.memset(zero[:], 0.0)
+        nc.vector.memset(w2_sc[:].bitcast(I32), 0)
+        nc.vector.memset(placed[0][:], 0.0)
+
+        def load_w1(g):
+            rows = w1[g * P * PACK : (g + 1) * P * PACK, :]
+            nc.sync.dma_start(out=w1_raw[g][:], in_=rows.rearrange("(p j) c -> p j c", j=PACK))
+
+        def load_x(g):
+            nc.sync.dma_start(out=x_win[g][:], in_=x_words[g].rearrange("p n t -> p (n t)").bitcast(I32))
+
+        for q in range(4):
+            nc.sync.dma_start(
+                out=xs_rows[32 * q : 32 * q + 4 * PASSES, :],
+                in_=x_scales[:, 4 * q : 4 * q + 4, :].bitcast(I32),
+            )
+        load_w1(0)
+        nc.sync.dma_start(offs_sb[:], offs)
+        load_w1(1)
+        nc.sync.dma_start(dst_sb[:], dst)
+        load_x(0)
+        load_x(1)
+        nc.sync.dma_start(out=w2_codes[:], in_=w2_words[0].rearrange("p n t -> p (n t)").bitcast(I32))
+        for q in range(4):
+            nc.sync.dma_start(
+                out=w2_sc[32 * q : 32 * q + 4, :].bitcast(I32),
+                in_=w2_scales[0, 4 * q : 4 * q + 4, :].bitcast(I32),
+            )
+        nc.sync.dma_start(out=gate_sb[:], in_=gate)
+
+        def entries(tile, a, b):
+            return tile[:, a // LANES : b // LANES]
+
+        def gather_words(g, a, b):
+            nc.vector.tensor_copy(
+                out=x_pick[g][:, a:b], in_=x_win[g][:].bitcast(U32).indirect(entries(offs_sb, a, b))
+            )
+
+        def weave_views(g, a, b):
+            return (
+                w1_bf[g][:].rearrange("p (t m j) -> p m j t", t=PACK, j=PACK)[:, a:b],
+                w1_raw[g][:].rearrange("p j (m t) -> p m j t", t=PACK)[:, a:b],
+            )
+
+        def quantize_w1(g):
+            nc.vector.quantize_mx(out=w1_codes[g][:].bitcast(FP8X4), scales=w1_sc[g][:], in_=w1_bf[g][:])
+
+        def h_pass(i, t, g):
+            cols = slice(i * TILE, (i + 1) * TILE)
+            chans = slice(t * P, (t + 1) * P)
+            nc.tensor.matmul_mx(
+                out=banks[i][:, t * TILE : (t + 1) * TILE],
+                lhsT=w1_codes[g][:, chans].bitcast(FP8X4),
+                lhsT_scale=w1_sc[g][:, chans],
+                rhs=x_pick[g][:, cols].bitcast(FP8X4),
+                rhs_scale=xs_pick[4 * g :, cols],
+                start=(g == 0),
+                stop=(g == PASSES - 1),
+            )
+
+        def h_tile(i):
+            h_pass(i, 0, 1)
+            for t in range(1, PACK):
+                for g in range(PASSES):
+                    h_pass(i, t, g)
+            nc.scalar.activation(
+                out=h_bf[:, i * PACK * TILE : (i + 1) * PACK * TILE].rearrange("p (n t) -> p n t", t=PACK),
+                in_=banks[i][:].rearrange("p (t n) -> p n t", t=PACK),
+                func=RELU,
+            )
+
+        def quantize_h(c):
+            cols = slice(c * CHUNK, (c + 1) * CHUNK)
+            nc.vector.quantize_mx(
+                out=h_codes[:, cols].bitcast(FP8X4),
+                scales=h_sc[:, cols],
+                in_=h_bf[:, c * PACK * CHUNK : (c + 1) * PACK * CHUNK],
+            )
+
+        def y_piece(b, a, e, bank):
+            rows = slice(b * P, (b + 1) * P)
+            nc.tensor.matmul_mx(
+                out=banks[bank][:, : e - a],
+                lhsT=w2_codes[:, rows].bitcast(FP8X4),
+                lhsT_scale=w2_sc[:, rows],
+                rhs=h_codes[:, a:e].bitcast(FP8X4),
+                rhs_scale=h_sc[:, a:e],
+                start=True,
+                stop=True,
+            )
+            nc.scalar.copy(out=y_sb[b][:, a:e], in_=banks[bank][:, : e - a])
+
+        def scatter(b, a, e):
+            nc.vector.tensor_tensor(
+                placed[b][:].indirect(entries(dst_sb, a, e)), y_sb[b][:, a:e], gate_sb[:, a:e], MULT
+            )
+
+        for q in range(4):
+            live = slice(32 * q, 32 * q + 4 * PASSES)
+            nc.vector.tensor_copy(out=xs_win[live, :].bitcast(I32), in_=xs_rows[live, :])
+        nc.vector.tensor_copy(out=xs_pick[:], in_=xs_win[:].indirect(offs_sb[:]))
+        o, i = weave_views(0, 0, P)
+        nc.scalar.copy(out=o, in_=i)
+        o, i = weave_views(1, 0, P // 2)
+        nc.vector.tensor_copy(out=o, in_=i)
+        o, i = weave_views(1, P // 2, P)
+        nc.scalar.copy(out=o, in_=i)
+        placed.append(keep.tile([P, U], F32, name="placed1", tag="stage1", align_bytes=64))
+        nc.scalar.activation(out=placed[1][:], in_=zero[:].to_broadcast([P, U]), func=RELU)
+        quantize_w1(0)
+        quantize_w1(1)
+        gather_words(0, 0, S // 2)
+        gather_words(0, S // 2, S)
+        for i in range(S // TILE):
+            h_pass(i, 0, 0)
+        gather_words(1, 0, CHUNK)
+        gather_words(1, CHUNK, S)
+
+        h_tile(0)
+        h_tile(1)
+        quantize_h(0)
+        h_tile(2)
+        y_piece(0, 0, CHUNK, 0)
+        scatter(0, 0, CHUNK)
+        h_tile(3)
+        quantize_h(1)
+        y_piece(1, 0, CHUNK, 3)
+        scatter(1, 0, CHUNK)
+        h_tile(4)
+        h_tile(5)
+        quantize_h(2)
+        y_piece(0, CHUNK, 2 * CHUNK, 5)
+        scatter(0, CHUNK, 2 * CHUNK)
+        h_tile(6)
+        h_tile(7)
+        quantize_h(3)
+        y_piece(0, 2 * CHUNK, 3 * CHUNK, 7)
+        scatter(0, 2 * CHUNK, 3 * CHUNK)
+        y_piece(0, 3 * CHUNK, S, 1)
+        scatter(0, 3 * CHUNK, S)
+        nc.sync.dma_start(out=out[0:P, :], in_=placed[0][:])
+        y_piece(1, CHUNK, 3 * CHUNK, 2)
+        y_piece(1, 3 * CHUNK, S, 4)
+        scatter(1, CHUNK, S)
+        nc.sync.dma_start(out=out[P : 2 * P, :], in_=placed[1][:])

@@ -21,6 +21,7 @@ PASSES = K // (P * PACK)
 TILE = 128
 CHUNK = 256
 LANES = 16
+OPENED = (S - CHUNK) // TILE
 
 
 def tile_picked_route2_mlprelu_p_kernel(tc, x_words, x_scales, gate, w1, w2_words, w2_scales, offs, dst, out):
@@ -34,6 +35,8 @@ def tile_picked_route2_mlprelu_p_kernel(tc, x_words, x_scales, gate, w1, w2_word
         x_win = [keep.tile([P, T], I32, name="x_win%d" % g, align_bytes=64) for g in range(PASSES)]
         xs_win = keep.tile([P, T], U8, name="xs_win", align_bytes=64)
         x_pick = [keep.tile([P, S], U32, name="x_pick%d" % g, align_bytes=64) for g in range(PASSES)]
+        h_first = keep.tile([P, PACK * CHUNK], BF16, name="h_first", tag="reused", align_bytes=64)
+        late = []
         xs_pick = keep.tile([P, S], U8, name="xs_pick", align_bytes=64)
         w1_raw = [
             keep.tile([P, PACK, H], F32, name="w1_raw%d" % g, tag="stage%d" % g, align_bytes=64)
@@ -74,9 +77,9 @@ def tile_picked_route2_mlprelu_p_kernel(tc, x_words, x_scales, gate, w1, w2_word
         load_w1(0)
         nc.sync.dma_start(offs_sb[:], offs)
         load_w1(1)
-        nc.sync.dma_start(dst_sb[:], dst)
         load_x(0)
         load_x(1)
+        nc.sync.dma_start(dst_sb[:], dst)
         nc.sync.dma_start(out=w2_codes[:], in_=w2_words[0].rearrange("p n t -> p (n t)").bitcast(I32))
         for q in range(4):
             nc.sync.dma_start(
@@ -88,9 +91,30 @@ def tile_picked_route2_mlprelu_p_kernel(tc, x_words, x_scales, gate, w1, w2_word
         def entries(tile, a, b):
             return tile[:, a // LANES : b // LANES]
 
+        def picked(g, a, b):
+            if g == 0 and a >= S - CHUNK:
+                return late[0][:, a - (S - CHUNK) : b - (S - CHUNK)]
+            return x_pick[g][:, a:b]
+
+        def h_values(a, b):
+            if b <= CHUNK:
+                return h_first[:, PACK * a : PACK * b]
+            return h_bf[:, PACK * a : PACK * b]
+
+        def warm(rhs, rhs_scale):
+            nc.tensor.matmul_mx(
+                out=banks[7][:],
+                lhsT=w1_codes[0][:, :P].bitcast(FP8X4),
+                lhsT_scale=w1_sc[0][:, :P],
+                rhs=rhs.bitcast(FP8X4),
+                rhs_scale=rhs_scale,
+                start=True,
+                stop=True,
+            )
+
         def gather_words(g, a, b):
             nc.vector.tensor_copy(
-                out=x_pick[g][:, a:b], in_=x_win[g][:].bitcast(U32).indirect(entries(offs_sb, a, b))
+                out=picked(g, a, b), in_=x_win[g][:].bitcast(U32).indirect(entries(offs_sb, a, b))
             )
 
         def weave_views(g, a, b):
@@ -109,19 +133,21 @@ def tile_picked_route2_mlprelu_p_kernel(tc, x_words, x_scales, gate, w1, w2_word
                 out=banks[i][:, t * TILE : (t + 1) * TILE],
                 lhsT=w1_codes[g][:, chans].bitcast(FP8X4),
                 lhsT_scale=w1_sc[g][:, chans],
-                rhs=x_pick[g][:, cols].bitcast(FP8X4),
+                rhs=picked(g, i * TILE, (i + 1) * TILE).bitcast(FP8X4),
                 rhs_scale=xs_pick[4 * g :, cols],
                 start=(g == 0),
                 stop=(g == PASSES - 1),
             )
 
         def h_tile(i):
+            if i >= OPENED:
+                h_pass(i, 0, 0)
             h_pass(i, 0, 1)
             for t in range(1, PACK):
                 for g in range(PASSES):
                     h_pass(i, t, g)
             nc.scalar.activation(
-                out=h_bf[:, i * PACK * TILE : (i + 1) * PACK * TILE].rearrange("p (n t) -> p n t", t=PACK),
+                out=h_values(i * TILE, (i + 1) * TILE).rearrange("p (n t) -> p n t", t=PACK),
                 in_=banks[i][:].rearrange("p (t n) -> p n t", t=PACK),
                 func=RELU,
             )
@@ -131,10 +157,10 @@ def tile_picked_route2_mlprelu_p_kernel(tc, x_words, x_scales, gate, w1, w2_word
             nc.vector.quantize_mx(
                 out=h_codes[:, cols].bitcast(FP8X4),
                 scales=h_sc[:, cols],
-                in_=h_bf[:, c * PACK * CHUNK : (c + 1) * PACK * CHUNK],
+                in_=h_values(c * CHUNK, (c + 1) * CHUNK),
             )
 
-        def y_piece(b, a, e, bank):
+        def y_piece(b, a, e, bank, copy):
             rows = slice(b * P, (b + 1) * P)
             nc.tensor.matmul_mx(
                 out=banks[bank][:, : e - a],
@@ -145,7 +171,7 @@ def tile_picked_route2_mlprelu_p_kernel(tc, x_words, x_scales, gate, w1, w2_word
                 start=True,
                 stop=True,
             )
-            nc.scalar.copy(out=y_sb[b][:, a:e], in_=banks[bank][:, : e - a])
+            copy(out=y_sb[b][:, a:e], in_=banks[bank][:, : e - a])
 
         def scatter(b, a, e):
             nc.vector.tensor_tensor(
@@ -165,38 +191,39 @@ def tile_picked_route2_mlprelu_p_kernel(tc, x_words, x_scales, gate, w1, w2_word
         placed.append(keep.tile([P, U], F32, name="placed1", tag="stage1", align_bytes=64))
         nc.scalar.activation(out=placed[1][:], in_=zero[:].to_broadcast([P, U]), func=RELU)
         quantize_w1(0)
+        warm(w1_codes[0][:], w1_sc[0][:])
+        warm(w1_codes[0][:], w1_sc[0][:])
         quantize_w1(1)
-        gather_words(0, 0, S // 2)
-        gather_words(0, S // 2, S)
-        for i in range(S // TILE):
+        warm(w1_codes[1][:], w1_sc[1][:])
+        warm(w1_codes[1][:], w1_sc[1][:])
+        gather_words(0, 0, 2 * CHUNK)
+        for i in range(4):
+            h_pass(i, 0, 0)
+        warm(x_pick[0][:, : 2 * CHUNK], xs_pick[:, : 2 * CHUNK])
+        gather_words(0, 2 * CHUNK, 3 * CHUNK)
+        for i in range(4, OPENED):
             h_pass(i, 0, 0)
         gather_words(1, 0, CHUNK)
-        gather_words(1, CHUNK, S)
+        gather_words(1, CHUNK, 2 * CHUNK)
+        gather_words(1, 2 * CHUNK, S)
 
         h_tile(0)
         h_tile(1)
         quantize_h(0)
-        h_tile(2)
-        y_piece(0, 0, CHUNK, 0)
-        scatter(0, 0, CHUNK)
-        h_tile(3)
-        quantize_h(1)
-        y_piece(1, 0, CHUNK, 3)
-        scatter(1, 0, CHUNK)
-        h_tile(4)
-        h_tile(5)
-        quantize_h(2)
-        y_piece(0, CHUNK, 2 * CHUNK, 5)
-        scatter(0, CHUNK, 2 * CHUNK)
-        h_tile(6)
-        h_tile(7)
-        quantize_h(3)
-        y_piece(0, 2 * CHUNK, 3 * CHUNK, 7)
-        scatter(0, 2 * CHUNK, 3 * CHUNK)
-        y_piece(0, 3 * CHUNK, S, 1)
-        scatter(0, 3 * CHUNK, S)
+        late.append(keep.tile([P, CHUNK], U32, name="x_late", tag="reused", align_bytes=64))
+        gather_words(0, S - CHUNK, S)
+        y_piece(0, 0, CHUNK, 0, nc.vector.tensor_copy)
+        for c in range(1, S // CHUNK):
+            h_tile(2 * c)
+            h_tile(2 * c + 1)
+            if c > 1:
+                y_piece(0, (c - 1) * CHUNK, c * CHUNK, 2 * c + 1, nc.scalar.copy)
+            quantize_h(c)
+            scatter(0, (c - 1) * CHUNK, c * CHUNK)
+        y_piece(0, S - CHUNK, S, 1, nc.scalar.copy)
+        scatter(0, S - CHUNK, S)
         nc.sync.dma_start(out=out[0:P, :], in_=placed[0][:])
-        y_piece(1, CHUNK, 3 * CHUNK, 2)
-        y_piece(1, 3 * CHUNK, S, 4)
-        scatter(1, CHUNK, S)
+        y_piece(1, 0, S // 2, 6, nc.scalar.copy)
+        y_piece(1, S // 2, S, 2, nc.scalar.copy)
+        scatter(1, 0, S)
         nc.sync.dma_start(out=out[P : 2 * P, :], in_=placed[1][:])

@@ -57,10 +57,10 @@ def tile_picked_route2_mlprelu_p_kernel(tc, x_words, x_scales, gate, w1, w2_word
         zero = keep.tile([P, 1], F32, name="zero")
         banks = [psum.tile([P, PACK * TILE], F32, name="bank%d" % i) for i in range(S // TILE)]
 
-        nc.vector.memset(xs_win[:].bitcast(I32), 0)
         nc.vector.memset(zero[:], 0.0)
+        nc.vector.memset(xs_win[:].bitcast(I32), 0)
         nc.vector.memset(w2_sc[:].bitcast(I32), 0)
-        nc.vector.memset(placed[0][:], 0.0)
+        nc.scalar.activation(out=placed[0][:], in_=zero[:].to_broadcast([P, U]), func=RELU)
 
         def load_w1(g):
             rows = w1[g * P * PACK : (g + 1) * P * PACK, :]
@@ -77,9 +77,9 @@ def tile_picked_route2_mlprelu_p_kernel(tc, x_words, x_scales, gate, w1, w2_word
         load_w1(0)
         nc.sync.dma_start(offs_sb[:], offs)
         load_w1(1)
+        nc.sync.dma_start(dst_sb[:], dst)
         load_x(0)
         load_x(1)
-        nc.sync.dma_start(dst_sb[:], dst)
         nc.sync.dma_start(out=w2_codes[:], in_=w2_words[0].rearrange("p n t -> p (n t)").bitcast(I32))
         for q in range(4):
             nc.sync.dma_start(
@@ -119,8 +119,8 @@ def tile_picked_route2_mlprelu_p_kernel(tc, x_words, x_scales, gate, w1, w2_word
 
         def weave_views(g, a, b):
             return (
-                w1_bf[g][:].rearrange("p (t m j) -> p m j t", t=PACK, j=PACK)[:, a:b],
-                w1_raw[g][:].rearrange("p j (m t) -> p m j t", t=PACK)[:, a:b],
+                w1_bf[g][:].rearrange("p (t m j) -> p m t j", t=PACK, j=PACK)[:, a:b],
+                w1_raw[g][:].rearrange("p j (m t) -> p m t j", t=PACK)[:, a:b],
             )
 
         def quantize_w1(g):

@@ -14,6 +14,7 @@ U8 = mybir.dt.uint8
 FP8X4 = mybir.dt.float8_e4m3fn_x4
 RELU = mybir.ActivationFunctionType.Relu
 MULT = mybir.AluOpType.mult
+ADD = mybir.AluOpType.add
 
 P = 128
 PACK = 4
@@ -21,7 +22,9 @@ PASSES = K // (P * PACK)
 TILE = 128
 CHUNK = 256
 LANES = 16
-OPENED = (S - CHUNK) // TILE
+SHARE = (48, 64)
+OPENED = 4
+H_BANK = (0, 1, 2, 3, 4, 5, 2, 3)
 
 
 def tile_picked_route2_mlprelu_p_kernel(tc, x_words, x_scales, gate, w1, w2_words, w2_scales, offs, dst, out):
@@ -35,8 +38,6 @@ def tile_picked_route2_mlprelu_p_kernel(tc, x_words, x_scales, gate, w1, w2_word
         x_win = [keep.tile([P, T], I32, name="x_win%d" % g, align_bytes=64) for g in range(PASSES)]
         xs_win = keep.tile([P, T], U8, name="xs_win", align_bytes=64)
         x_pick = [keep.tile([P, S], U32, name="x_pick%d" % g, align_bytes=64) for g in range(PASSES)]
-        h_first = keep.tile([P, PACK * CHUNK], BF16, name="h_first", tag="reused", align_bytes=64)
-        late = []
         xs_pick = keep.tile([P, S], U8, name="xs_pick", align_bytes=64)
         w1_raw = [
             keep.tile([P, PACK, H], F32, name="w1_raw%d" % g, tag="stage%d" % g, align_bytes=64)
@@ -54,13 +55,13 @@ def tile_picked_route2_mlprelu_p_kernel(tc, x_words, x_scales, gate, w1, w2_word
         h_sc = keep.tile([P, S], U8, name="h_sc", align_bytes=64)
         y_sb = [keep.tile([P, S], F32, name="y_sb%d" % b, align_bytes=64) for b in range(N // P)]
         placed = [keep.tile([P, U], F32, name="placed0", align_bytes=64)]
-        zero = keep.tile([P, 1], F32, name="zero")
+        zero = keep.tile([P, TILE], F32, name="zero", align_bytes=64)
         banks = [psum.tile([P, PACK * TILE], F32, name="bank%d" % i) for i in range(S // TILE)]
 
         nc.vector.memset(zero[:], 0.0)
         nc.vector.memset(xs_win[:].bitcast(I32), 0)
         nc.vector.memset(w2_sc[:].bitcast(I32), 0)
-        nc.scalar.activation(out=placed[0][:], in_=zero[:].to_broadcast([P, U]), func=RELU)
+        nc.scalar.activation(out=placed[0][:], in_=zero[:, 0:1].to_broadcast([P, U]), func=RELU)
 
         def load_w1(g):
             rows = w1[g * P * PACK : (g + 1) * P * PACK, :]
@@ -69,45 +70,48 @@ def tile_picked_route2_mlprelu_p_kernel(tc, x_words, x_scales, gate, w1, w2_word
         def load_x(g):
             nc.sync.dma_start(out=x_win[g][:], in_=x_words[g].rearrange("p n t -> p (n t)").bitcast(I32))
 
-        for q in range(4):
+        for q in range(2):
             nc.sync.dma_start(
                 out=xs_rows[32 * q : 32 * q + 4 * PASSES, :],
                 in_=x_scales[:, 4 * q : 4 * q + 4, :].bitcast(I32),
             )
-        load_w1(0)
+        for q in range(2, 4):
+            for g in range(PASSES):
+                nc.sync.dma_start(
+                    out=xs_rows[32 * q + 4 * g : 32 * q + 4 * g + 4, :],
+                    in_=x_scales[g, 4 * q : 4 * q + 4, :].bitcast(I32),
+                )
         nc.sync.dma_start(offs_sb[:], offs)
-        load_w1(1)
-        nc.sync.dma_start(dst_sb[:], dst)
+        load_w1(0)
         load_x(0)
-        load_x(1)
-        nc.sync.dma_start(out=w2_codes[:], in_=w2_words[0].rearrange("p n t -> p (n t)").bitcast(I32))
+        nc.sync.dma_start(dst_sb[:], dst)
+        load_w1(1)
         for q in range(4):
             nc.sync.dma_start(
                 out=w2_sc[32 * q : 32 * q + 4, :].bitcast(I32),
                 in_=w2_scales[0, 4 * q : 4 * q + 4, :].bitcast(I32),
             )
-        nc.sync.dma_start(out=gate_sb[:], in_=gate)
+        load_x(1)
+        nc.sync.dma_start(out=w2_codes[:], in_=w2_words[0].rearrange("p n t -> p (n t)").bitcast(I32))
+        nc.sync.dma_start(out=gate_sb[:, :CHUNK], in_=gate[:, :CHUNK])
+        nc.sync.dma_start(out=gate_sb[:, CHUNK:], in_=gate[:, CHUNK:])
 
         def entries(tile, a, b):
             return tile[:, a // LANES : b // LANES]
 
         def picked(g, a, b):
-            if g == 0 and a >= S - CHUNK:
-                return late[0][:, a - (S - CHUNK) : b - (S - CHUNK)]
             return x_pick[g][:, a:b]
 
         def h_values(a, b):
-            if b <= CHUNK:
-                return h_first[:, PACK * a : PACK * b]
             return h_bf[:, PACK * a : PACK * b]
 
-        def warm(rhs, rhs_scale):
+        def warm(codes, scales):
             nc.tensor.matmul_mx(
                 out=banks[7][:],
-                lhsT=w1_codes[0][:, :P].bitcast(FP8X4),
-                lhsT_scale=w1_sc[0][:, :P],
-                rhs=rhs.bitcast(FP8X4),
-                rhs_scale=rhs_scale,
+                lhsT=codes.bitcast(FP8X4),
+                lhsT_scale=scales,
+                rhs=w1_codes[0][:].bitcast(FP8X4),
+                rhs_scale=w1_sc[0][:],
                 start=True,
                 stop=True,
             )
@@ -119,9 +123,13 @@ def tile_picked_route2_mlprelu_p_kernel(tc, x_words, x_scales, gate, w1, w2_word
 
         def weave_views(g, a, b):
             return (
-                w1_bf[g][:].rearrange("p (t m j) -> p m t j", t=PACK, j=PACK)[:, a:b],
-                w1_raw[g][:].rearrange("p j (m t) -> p m t j", t=PACK)[:, a:b],
+                w1_bf[g][:].rearrange("p (t m j) -> p m j t", t=PACK, j=PACK)[:, a:b],
+                w1_raw[g][:].rearrange("p j (m t) -> p m j t", t=PACK)[:, a:b],
             )
+
+        def weave(g, a, b, copy):
+            o, i = weave_views(g, a, b)
+            copy(out=o, in_=i)
 
         def quantize_w1(g):
             nc.vector.quantize_mx(out=w1_codes[g][:].bitcast(FP8X4), scales=w1_sc[g][:], in_=w1_bf[g][:])
@@ -130,7 +138,7 @@ def tile_picked_route2_mlprelu_p_kernel(tc, x_words, x_scales, gate, w1, w2_word
             cols = slice(i * TILE, (i + 1) * TILE)
             chans = slice(t * P, (t + 1) * P)
             nc.tensor.matmul_mx(
-                out=banks[i][:, t * TILE : (t + 1) * TILE],
+                out=banks[H_BANK[i]][:, t * TILE : (t + 1) * TILE],
                 lhsT=w1_codes[g][:, chans].bitcast(FP8X4),
                 lhsT_scale=w1_sc[g][:, chans],
                 rhs=picked(g, i * TILE, (i + 1) * TILE).bitcast(FP8X4),
@@ -148,22 +156,19 @@ def tile_picked_route2_mlprelu_p_kernel(tc, x_words, x_scales, gate, w1, w2_word
                     h_pass(i, t, g)
             nc.scalar.activation(
                 out=h_values(i * TILE, (i + 1) * TILE).rearrange("p (n t) -> p n t", t=PACK),
-                in_=banks[i][:].rearrange("p (t n) -> p n t", t=PACK),
+                in_=banks[H_BANK[i]][:].rearrange("p (t n) -> p n t", t=PACK),
                 func=RELU,
             )
 
-        def quantize_h(c):
-            cols = slice(c * CHUNK, (c + 1) * CHUNK)
+        def quantize_h(a, b):
             nc.vector.quantize_mx(
-                out=h_codes[:, cols].bitcast(FP8X4),
-                scales=h_sc[:, cols],
-                in_=h_values(c * CHUNK, (c + 1) * CHUNK),
+                out=h_codes[:, a:b].bitcast(FP8X4), scales=h_sc[:, a:b], in_=h_values(a, b)
             )
 
-        def y_piece(b, a, e, bank, copy):
+        def y_pass(b, a, e, bank, at):
             rows = slice(b * P, (b + 1) * P)
             nc.tensor.matmul_mx(
-                out=banks[bank][:, : e - a],
+                out=banks[bank][:, at : at + e - a],
                 lhsT=w2_codes[:, rows].bitcast(FP8X4),
                 lhsT_scale=w2_sc[:, rows],
                 rhs=h_codes[:, a:e].bitcast(FP8X4),
@@ -171,7 +176,9 @@ def tile_picked_route2_mlprelu_p_kernel(tc, x_words, x_scales, gate, w1, w2_word
                 start=True,
                 stop=True,
             )
-            copy(out=y_sb[b][:, a:e], in_=banks[bank][:, : e - a])
+
+        def y_copy(b, a, e, bank):
+            nc.scalar.copy(out=y_sb[b][:, a:e], in_=banks[bank][:, : e - a])
 
         def scatter(b, a, e):
             nc.vector.tensor_tensor(
@@ -182,48 +189,58 @@ def tile_picked_route2_mlprelu_p_kernel(tc, x_words, x_scales, gate, w1, w2_word
             live = slice(32 * q, 32 * q + 4 * PASSES)
             nc.vector.tensor_copy(out=xs_win[live, :].bitcast(I32), in_=xs_rows[live, :])
         nc.vector.tensor_copy(out=xs_pick[:], in_=xs_win[:].indirect(offs_sb[:]))
-        o, i = weave_views(0, 0, P)
-        nc.scalar.copy(out=o, in_=i)
-        o, i = weave_views(1, 0, P // 2)
-        nc.vector.tensor_copy(out=o, in_=i)
-        o, i = weave_views(1, P // 2, P)
-        nc.scalar.copy(out=o, in_=i)
-        placed.append(keep.tile([P, U], F32, name="placed1", tag="stage1", align_bytes=64))
-        nc.scalar.activation(out=placed[1][:], in_=zero[:].to_broadcast([P, U]), func=RELU)
+        weave(0, 0, SHARE[0], nc.vector.tensor_copy)
+        weave(0, SHARE[0], P, nc.scalar.copy)
+        placed.append(keep.tile([P, U], F32, name="placed1", tag="stage0", align_bytes=64))
+        nc.scalar.activation(out=placed[1][:], in_=zero[:, 0:1].to_broadcast([P, U]), func=RELU)
+        gather_words(0, 0, S // 2)
         quantize_w1(0)
-        warm(w1_codes[0][:], w1_sc[0][:])
-        warm(w1_codes[0][:], w1_sc[0][:])
+        for i in range(OPENED):
+            h_pass(i, 0, 0)
+        warm(x_pick[0][:, :P], xs_pick[:, :P])
+        gather_words(0, S // 2, S)
+        warm(x_pick[0][:, S - P :], xs_pick[:, S - P :])
+        warm(x_pick[0][:, S - P :], xs_pick[:, S - P :])
+        weave(1, 0, SHARE[1], nc.vector.tensor_copy)
+        weave(1, SHARE[1], P, nc.scalar.copy)
         quantize_w1(1)
-        warm(w1_codes[1][:], w1_sc[1][:])
-        warm(w1_codes[1][:], w1_sc[1][:])
-        gather_words(0, 0, 2 * CHUNK)
-        for i in range(4):
-            h_pass(i, 0, 0)
-        warm(x_pick[0][:, : 2 * CHUNK], xs_pick[:, : 2 * CHUNK])
-        gather_words(0, 2 * CHUNK, 3 * CHUNK)
-        for i in range(4, OPENED):
-            h_pass(i, 0, 0)
+        warm(w1_codes[1][:, :P], w1_sc[1][:, :P])
+        warm(w1_codes[1][:, :P], w1_sc[1][:, :P])
         gather_words(1, 0, CHUNK)
         gather_words(1, CHUNK, 2 * CHUNK)
         gather_words(1, 2 * CHUNK, S)
 
         h_tile(0)
+        quantize_h(0, TILE)
+        y_pass(0, 0, TILE, 4, 0)
+        first = keep.tile([P, TILE], F32, name="first", align_bytes=64)
+        nc.vector.tensor_tensor(first[:], banks[4][:, :TILE], gate_sb[:, :TILE], MULT)
         h_tile(1)
-        quantize_h(0)
-        late.append(keep.tile([P, CHUNK], U32, name="x_late", tag="reused", align_bytes=64))
-        gather_words(0, S - CHUNK, S)
-        y_piece(0, 0, CHUNK, 0, nc.vector.tensor_copy)
-        for c in range(1, S // CHUNK):
-            h_tile(2 * c)
-            h_tile(2 * c + 1)
-            if c > 1:
-                y_piece(0, (c - 1) * CHUNK, c * CHUNK, 2 * c + 1, nc.scalar.copy)
-            quantize_h(c)
-            scatter(0, (c - 1) * CHUNK, c * CHUNK)
-        y_piece(0, S - CHUNK, S, 1, nc.scalar.copy)
-        scatter(0, S - CHUNK, S)
+        quantize_h(TILE, CHUNK)
+        nc.vector.tensor_tensor(placed[0][:].indirect(entries(dst_sb, 0, TILE)), first[:], zero[:], ADD)
+        y_pass(1, 0, CHUNK, 5, 0)
+        h_tile(2)
+        h_tile(3)
+        quantize_h(CHUNK, 2 * CHUNK)
+        y_copy(1, 0, CHUNK, 5)
+        scatter(1, 0, CHUNK)
+        y_pass(0, TILE, CHUNK, 0, 0)
+        y_pass(0, CHUNK, 2 * CHUNK, 0, TILE)
+        y_copy(0, TILE, 2 * CHUNK, 0)
+        scatter(0, TILE, 2 * CHUNK)
+        for i in range(4, 8):
+            h_tile(i)
+        quantize_h(2 * CHUNK, S)
+        y_pass(1, CHUNK, 2 * CHUNK, 3, 0)
+        y_copy(1, CHUNK, 2 * CHUNK, 3)
+        scatter(1, CHUNK, 2 * CHUNK)
+        y_pass(0, 2 * CHUNK, 3 * CHUNK, 6, 0)
+        y_copy(0, 2 * CHUNK, 3 * CHUNK, 6)
+        y_pass(0, 3 * CHUNK, S, 0, 0)
+        y_copy(0, 3 * CHUNK, S, 0)
+        scatter(0, 2 * CHUNK, S)
         nc.sync.dma_start(out=out[0:P, :], in_=placed[0][:])
-        y_piece(1, 0, S // 2, 6, nc.scalar.copy)
-        y_piece(1, S // 2, S, 2, nc.scalar.copy)
-        scatter(1, 0, S)
+        y_pass(1, 2 * CHUNK, S, 7, 0)
+        y_copy(1, 2 * CHUNK, S, 7)
+        scatter(1, 2 * CHUNK, S)
         nc.sync.dma_start(out=out[P : 2 * P, :], in_=placed[1][:])

@@ -23,8 +23,6 @@ TILE = 128
 CHUNK = 256
 LANES = 16
 SHARE = (48, 64)
-OPENED = 4
-H_BANK = (0, 1, 2, 3, 4, 5, 2, 3)
 
 
 def tile_picked_route2_mlprelu_p_kernel(tc, x_words, x_scales, gate, w1, w2_words, w2_scales, offs, dst, out):
@@ -37,7 +35,8 @@ def tile_picked_route2_mlprelu_p_kernel(tc, x_words, x_scales, gate, w1, w2_word
         dst_sb = keep.tile([P, S // LANES], U16, name="dst_sb")
         x_win = [keep.tile([P, T], I32, name="x_win%d" % g, align_bytes=64) for g in range(PASSES)]
         xs_win = keep.tile([P, T], U8, name="xs_win", align_bytes=64)
-        x_pick = [keep.tile([P, S], U32, name="x_pick%d" % g, align_bytes=64) for g in range(PASSES)]
+        x_pick = [keep.tile([P, S - g * CHUNK], U32, name="x_pick%d" % g, align_bytes=64) for g in range(PASSES)]
+        bias0 = keep.tile([P, 1], F32, name="bias0", tag="late", align_bytes=64)
         xs_pick = keep.tile([P, S], U8, name="xs_pick", align_bytes=64)
         w1_raw = [
             keep.tile([P, PACK, H], F32, name="w1_raw%d" % g, tag="stage%d" % g, align_bytes=64)
@@ -59,6 +58,7 @@ def tile_picked_route2_mlprelu_p_kernel(tc, x_words, x_scales, gate, w1, w2_word
         banks = [psum.tile([P, PACK * TILE], F32, name="bank%d" % i) for i in range(S // TILE)]
 
         nc.vector.memset(zero[:], 0.0)
+        nc.vector.memset(bias0[:], 0.0)
         nc.vector.memset(xs_win[:].bitcast(I32), 0)
         nc.vector.memset(w2_sc[:].bitcast(I32), 0)
         nc.scalar.activation(out=placed[0][:], in_=zero[:, 0:1].to_broadcast([P, U]), func=RELU)
@@ -84,7 +84,6 @@ def tile_picked_route2_mlprelu_p_kernel(tc, x_words, x_scales, gate, w1, w2_word
         nc.sync.dma_start(offs_sb[:], offs)
         load_w1(0)
         load_x(0)
-        nc.sync.dma_start(dst_sb[:], dst)
         load_w1(1)
         for q in range(4):
             nc.sync.dma_start(
@@ -93,28 +92,25 @@ def tile_picked_route2_mlprelu_p_kernel(tc, x_words, x_scales, gate, w1, w2_word
             )
         load_x(1)
         nc.sync.dma_start(out=w2_codes[:], in_=w2_words[0].rearrange("p n t -> p (n t)").bitcast(I32))
-        nc.sync.dma_start(out=gate_sb[:, :CHUNK], in_=gate[:, :CHUNK])
-        nc.sync.dma_start(out=gate_sb[:, CHUNK:], in_=gate[:, CHUNK:])
+        nc.sync.dma_start(out=gate_sb[:, :TILE], in_=gate[:, :TILE])
+        nc.sync.dma_start(dst_sb[:], dst)
+        nc.sync.dma_start(out=gate_sb[:, TILE:], in_=gate[:, TILE:])
 
         def entries(tile, a, b):
             return tile[:, a // LANES : b // LANES]
 
         def picked(g, a, b):
+            if g == 1 and a >= S - CHUNK:
+                return x_pick[2][:, a - (S - CHUNK) : b - (S - CHUNK)]
             return x_pick[g][:, a:b]
+
+        def h_scales(a, b):
+            if a == TILE:
+                return h_sc[4:, :TILE]
+            return h_sc[:, a:b]
 
         def h_values(a, b):
             return h_bf[:, PACK * a : PACK * b]
-
-        def warm(codes, scales):
-            nc.tensor.matmul_mx(
-                out=banks[7][:],
-                lhsT=codes.bitcast(FP8X4),
-                lhsT_scale=scales,
-                rhs=w1_codes[0][:].bitcast(FP8X4),
-                rhs_scale=w1_sc[0][:],
-                start=True,
-                stop=True,
-            )
 
         def gather_words(g, a, b):
             nc.vector.tensor_copy(
@@ -138,31 +134,32 @@ def tile_picked_route2_mlprelu_p_kernel(tc, x_words, x_scales, gate, w1, w2_word
             cols = slice(i * TILE, (i + 1) * TILE)
             chans = slice(t * P, (t + 1) * P)
             nc.tensor.matmul_mx(
-                out=banks[H_BANK[i]][:, t * TILE : (t + 1) * TILE],
+                out=banks[i][:, t * TILE : (t + 1) * TILE],
                 lhsT=w1_codes[g][:, chans].bitcast(FP8X4),
                 lhsT_scale=w1_sc[g][:, chans],
                 rhs=picked(g, i * TILE, (i + 1) * TILE).bitcast(FP8X4),
                 rhs_scale=xs_pick[4 * g :, cols],
-                start=(g == 0),
-                stop=(g == PASSES - 1),
+                start=(g == 0 and t == 0),
+                stop=(g == PASSES - 1 and t == PACK - 1),
             )
 
-        def h_tile(i):
-            if i >= OPENED:
-                h_pass(i, 0, 0)
-            h_pass(i, 0, 1)
-            for t in range(1, PACK):
-                for g in range(PASSES):
-                    h_pass(i, t, g)
+        def open_tile(i):
+            for t in range(PACK):
+                h_pass(i, t, 0)
+
+        def h_tile(i, bias=0.0):
+            for t in range(PACK):
+                h_pass(i, t, 1)
             nc.scalar.activation(
                 out=h_values(i * TILE, (i + 1) * TILE).rearrange("p (n t) -> p n t", t=PACK),
-                in_=banks[H_BANK[i]][:].rearrange("p (t n) -> p n t", t=PACK),
+                in_=banks[i][:].rearrange("p (t n) -> p n t", t=PACK),
                 func=RELU,
+                bias=bias,
             )
 
         def quantize_h(a, b):
             nc.vector.quantize_mx(
-                out=h_codes[:, a:b].bitcast(FP8X4), scales=h_sc[:, a:b], in_=h_values(a, b)
+                out=h_codes[:, a:b].bitcast(FP8X4), scales=h_scales(a, b), in_=h_values(a, b)
             )
 
         def y_pass(b, a, e, bank, at):
@@ -172,7 +169,7 @@ def tile_picked_route2_mlprelu_p_kernel(tc, x_words, x_scales, gate, w1, w2_word
                 lhsT=w2_codes[:, rows].bitcast(FP8X4),
                 lhsT_scale=w2_sc[:, rows],
                 rhs=h_codes[:, a:e].bitcast(FP8X4),
-                rhs_scale=h_sc[:, a:e],
+                rhs_scale=h_scales(a, e),
                 start=True,
                 stop=True,
             )
@@ -193,54 +190,52 @@ def tile_picked_route2_mlprelu_p_kernel(tc, x_words, x_scales, gate, w1, w2_word
         weave(0, SHARE[0], P, nc.scalar.copy)
         placed.append(keep.tile([P, U], F32, name="placed1", tag="stage0", align_bytes=64))
         nc.scalar.activation(out=placed[1][:], in_=zero[:, 0:1].to_broadcast([P, U]), func=RELU)
-        gather_words(0, 0, S // 2)
         quantize_w1(0)
-        for i in range(OPENED):
-            h_pass(i, 0, 0)
-        warm(x_pick[0][:, :P], xs_pick[:, :P])
-        gather_words(0, S // 2, S)
-        warm(x_pick[0][:, S - P :], xs_pick[:, S - P :])
-        warm(x_pick[0][:, S - P :], xs_pick[:, S - P :])
+        for a, b in ((0, CHUNK), (CHUNK, 2 * CHUNK), (2 * CHUNK, S)):
+            gather_words(0, a, b)
+            for i in range(a // TILE, b // TILE):
+                open_tile(i)
         weave(1, 0, SHARE[1], nc.vector.tensor_copy)
         weave(1, SHARE[1], P, nc.scalar.copy)
         quantize_w1(1)
-        warm(w1_codes[1][:, :P], w1_sc[1][:, :P])
-        warm(w1_codes[1][:, :P], w1_sc[1][:, :P])
         gather_words(1, 0, CHUNK)
         gather_words(1, CHUNK, 2 * CHUNK)
-        gather_words(1, 2 * CHUNK, S)
+        gather_words(1, 2 * CHUNK, 3 * CHUNK)
 
-        h_tile(0)
+        h_tile(0, bias0[:])
         quantize_h(0, TILE)
-        y_pass(0, 0, TILE, 4, 0)
+        x_pick.append(keep.tile([P, CHUNK], U32, name="x_pick2", tag="late", align_bytes=64))
+        gather_words(1, 3 * CHUNK, S)
+        y_pass(0, 0, TILE, 0, 0)
         first = keep.tile([P, TILE], F32, name="first", align_bytes=64)
-        nc.vector.tensor_tensor(first[:], banks[4][:, :TILE], gate_sb[:, :TILE], MULT)
+        nc.vector.tensor_tensor(first[:], banks[0][:, :TILE], gate_sb[:, :TILE], MULT)
         h_tile(1)
         quantize_h(TILE, CHUNK)
         nc.vector.tensor_tensor(placed[0][:].indirect(entries(dst_sb, 0, TILE)), first[:], zero[:], ADD)
-        y_pass(1, 0, CHUNK, 5, 0)
+        y_pass(1, 0, TILE, 1, 0)
+        y_pass(1, TILE, CHUNK, 1, TILE)
         h_tile(2)
         h_tile(3)
         quantize_h(CHUNK, 2 * CHUNK)
-        y_copy(1, 0, CHUNK, 5)
+        y_copy(1, 0, CHUNK, 1)
         scatter(1, 0, CHUNK)
-        y_pass(0, TILE, CHUNK, 0, 0)
-        y_pass(0, CHUNK, 2 * CHUNK, 0, TILE)
-        y_copy(0, TILE, 2 * CHUNK, 0)
+        y_pass(0, TILE, CHUNK, 2, 0)
+        y_pass(0, CHUNK, 2 * CHUNK, 2, TILE)
+        y_copy(0, TILE, 2 * CHUNK, 2)
         scatter(0, TILE, 2 * CHUNK)
         for i in range(4, 8):
             h_tile(i)
         quantize_h(2 * CHUNK, S)
-        y_pass(1, CHUNK, 2 * CHUNK, 3, 0)
-        y_copy(1, CHUNK, 2 * CHUNK, 3)
+        y_pass(1, CHUNK, 2 * CHUNK, 7, 0)
+        y_copy(1, CHUNK, 2 * CHUNK, 7)
         scatter(1, CHUNK, 2 * CHUNK)
-        y_pass(0, 2 * CHUNK, 3 * CHUNK, 6, 0)
-        y_copy(0, 2 * CHUNK, 3 * CHUNK, 6)
-        y_pass(0, 3 * CHUNK, S, 0, 0)
-        y_copy(0, 3 * CHUNK, S, 0)
+        y_pass(0, 2 * CHUNK, 3 * CHUNK, 3, 0)
+        y_copy(0, 2 * CHUNK, 3 * CHUNK, 3)
+        y_pass(0, 3 * CHUNK, S, 4, 0)
+        y_copy(0, 3 * CHUNK, S, 4)
         scatter(0, 2 * CHUNK, S)
         nc.sync.dma_start(out=out[0:P, :], in_=placed[0][:])
-        y_pass(1, 2 * CHUNK, S, 7, 0)
-        y_copy(1, 2 * CHUNK, S, 7)
+        y_pass(1, 2 * CHUNK, S, 5, 0)
+        y_copy(1, 2 * CHUNK, S, 5)
         scatter(1, 2 * CHUNK, S)
         nc.sync.dma_start(out=out[P : 2 * P, :], in_=placed[1][:])

@@ -22,6 +22,8 @@ PASSES = K // (P * PACK)
 TILE = 128
 CHUNK = 256
 LANES = 16
+OPENED = 4
+H_BANK = (0, 1, 2, 3, 4, 5, 3, 0)
 SHARE = (48, 64)
 
 
@@ -104,13 +106,19 @@ def tile_picked_route2_mlprelu_p_kernel(tc, x_words, x_scales, gate, w1, w2_word
                 return x_pick[2][:, a - (S - CHUNK) : b - (S - CHUNK)]
             return x_pick[g][:, a:b]
 
-        def h_scales(a, b):
-            if a == TILE:
-                return h_sc[4:, :TILE]
-            return h_sc[:, a:b]
-
         def h_values(a, b):
             return h_bf[:, PACK * a : PACK * b]
+
+        def warm(codes, scales):
+            nc.tensor.matmul_mx(
+                out=banks[7][:],
+                lhsT=codes.bitcast(FP8X4),
+                lhsT_scale=scales,
+                rhs=w1_codes[0][:].bitcast(FP8X4),
+                rhs_scale=w1_sc[0][:],
+                start=True,
+                stop=True,
+            )
 
         def gather_words(g, a, b):
             nc.vector.tensor_copy(
@@ -134,7 +142,7 @@ def tile_picked_route2_mlprelu_p_kernel(tc, x_words, x_scales, gate, w1, w2_word
             cols = slice(i * TILE, (i + 1) * TILE)
             chans = slice(t * P, (t + 1) * P)
             nc.tensor.matmul_mx(
-                out=banks[i][:, t * TILE : (t + 1) * TILE],
+                out=banks[H_BANK[i]][:, t * TILE : (t + 1) * TILE],
                 lhsT=w1_codes[g][:, chans].bitcast(FP8X4),
                 lhsT_scale=w1_sc[g][:, chans],
                 rhs=picked(g, i * TILE, (i + 1) * TILE).bitcast(FP8X4),
@@ -148,18 +156,20 @@ def tile_picked_route2_mlprelu_p_kernel(tc, x_words, x_scales, gate, w1, w2_word
                 h_pass(i, t, 0)
 
         def h_tile(i, bias=0.0):
+            if i >= OPENED:
+                open_tile(i)
             for t in range(PACK):
                 h_pass(i, t, 1)
             nc.scalar.activation(
                 out=h_values(i * TILE, (i + 1) * TILE).rearrange("p (n t) -> p n t", t=PACK),
-                in_=banks[i][:].rearrange("p (t n) -> p n t", t=PACK),
+                in_=banks[H_BANK[i]][:].rearrange("p (t n) -> p n t", t=PACK),
                 func=RELU,
                 bias=bias,
             )
 
         def quantize_h(a, b):
             nc.vector.quantize_mx(
-                out=h_codes[:, a:b].bitcast(FP8X4), scales=h_scales(a, b), in_=h_values(a, b)
+                out=h_codes[:, a:b].bitcast(FP8X4), scales=h_sc[:, a:b], in_=h_values(a, b)
             )
 
         def y_pass(b, a, e, bank, at):
@@ -169,7 +179,7 @@ def tile_picked_route2_mlprelu_p_kernel(tc, x_words, x_scales, gate, w1, w2_word
                 lhsT=w2_codes[:, rows].bitcast(FP8X4),
                 lhsT_scale=w2_sc[:, rows],
                 rhs=h_codes[:, a:e].bitcast(FP8X4),
-                rhs_scale=h_scales(a, e),
+                rhs_scale=h_sc[:, a:e],
                 start=True,
                 stop=True,
             )
@@ -191,13 +201,19 @@ def tile_picked_route2_mlprelu_p_kernel(tc, x_words, x_scales, gate, w1, w2_word
         placed.append(keep.tile([P, U], F32, name="placed1", tag="stage0", align_bytes=64))
         nc.scalar.activation(out=placed[1][:], in_=zero[:, 0:1].to_broadcast([P, U]), func=RELU)
         quantize_w1(0)
-        for a, b in ((0, CHUNK), (CHUNK, 2 * CHUNK), (2 * CHUNK, S)):
-            gather_words(0, a, b)
-            for i in range(a // TILE, b // TILE):
+        warm(w1_codes[0][:, :P], w1_sc[0][:, :P])
+        for a in (0, CHUNK):
+            gather_words(0, a, a + CHUNK)
+            for i in range(a // TILE, (a + CHUNK) // TILE):
                 open_tile(i)
+        gather_words(0, S // 2, S)
+        warm(x_pick[0][:, S - P :], xs_pick[:, S - P :])
+        warm(x_pick[0][:, S - P :], xs_pick[:, S - P :])
         weave(1, 0, SHARE[1], nc.vector.tensor_copy)
         weave(1, SHARE[1], P, nc.scalar.copy)
         quantize_w1(1)
+        warm(w1_codes[1][:, :P], w1_sc[1][:, :P])
+        warm(w1_codes[1][:, :P], w1_sc[1][:, :P])
         gather_words(1, 0, CHUNK)
         gather_words(1, CHUNK, 2 * CHUNK)
         gather_words(1, 2 * CHUNK, 3 * CHUNK)
@@ -206,36 +222,36 @@ def tile_picked_route2_mlprelu_p_kernel(tc, x_words, x_scales, gate, w1, w2_word
         quantize_h(0, TILE)
         x_pick.append(keep.tile([P, CHUNK], U32, name="x_pick2", tag="late", align_bytes=64))
         gather_words(1, 3 * CHUNK, S)
-        y_pass(0, 0, TILE, 0, 0)
-        first = keep.tile([P, TILE], F32, name="first", align_bytes=64)
-        nc.vector.tensor_tensor(first[:], banks[0][:, :TILE], gate_sb[:, :TILE], MULT)
+        y_pass(0, 0, TILE, 4, 0)
         h_tile(1)
         quantize_h(TILE, CHUNK)
-        nc.vector.tensor_tensor(placed[0][:].indirect(entries(dst_sb, 0, TILE)), first[:], zero[:], ADD)
-        y_pass(1, 0, TILE, 1, 0)
-        y_pass(1, TILE, CHUNK, 1, TILE)
+        y_pass(1, 0, CHUNK, 5, 0)
+        first = keep.tile([P, TILE], F32, name="first", align_bytes=64)
+        nc.vector.tensor_tensor(first[:], banks[4][:, :TILE], gate_sb[:, :TILE], MULT)
         h_tile(2)
+        quantize_h(CHUNK, 3 * TILE)
+        nc.vector.tensor_tensor(placed[0][:].indirect(entries(dst_sb, 0, TILE)), first[:], zero[:], ADD)
         h_tile(3)
-        quantize_h(CHUNK, 2 * CHUNK)
-        y_copy(1, 0, CHUNK, 1)
+        quantize_h(3 * TILE, 2 * CHUNK)
+        y_copy(1, 0, CHUNK, 5)
         scatter(1, 0, CHUNK)
-        y_pass(0, TILE, CHUNK, 2, 0)
-        y_pass(0, CHUNK, 2 * CHUNK, 2, TILE)
-        y_copy(0, TILE, 2 * CHUNK, 2)
+        y_pass(0, TILE, CHUNK, 0, 0)
+        y_pass(0, CHUNK, 2 * CHUNK, 0, TILE)
+        y_copy(0, TILE, 2 * CHUNK, 0)
         scatter(0, TILE, 2 * CHUNK)
         for i in range(4, 8):
             h_tile(i)
         quantize_h(2 * CHUNK, S)
-        y_pass(1, CHUNK, 2 * CHUNK, 7, 0)
-        y_copy(1, CHUNK, 2 * CHUNK, 7)
+        y_pass(1, CHUNK, 2 * CHUNK, 0, 0)
+        y_copy(1, CHUNK, 2 * CHUNK, 0)
         scatter(1, CHUNK, 2 * CHUNK)
-        y_pass(0, 2 * CHUNK, 3 * CHUNK, 3, 0)
-        y_copy(0, 2 * CHUNK, 3 * CHUNK, 3)
-        y_pass(0, 3 * CHUNK, S, 4, 0)
-        y_copy(0, 3 * CHUNK, S, 4)
+        y_pass(0, 2 * CHUNK, 3 * CHUNK, 6, 0)
+        y_copy(0, 2 * CHUNK, 3 * CHUNK, 6)
+        y_pass(0, 3 * CHUNK, S, 1, 0)
+        y_copy(0, 3 * CHUNK, S, 1)
         scatter(0, 2 * CHUNK, S)
         nc.sync.dma_start(out=out[0:P, :], in_=placed[0][:])
-        y_pass(1, 2 * CHUNK, S, 5, 0)
-        y_copy(1, 2 * CHUNK, S, 5)
+        y_pass(1, 2 * CHUNK, S, 7, 0)
+        y_copy(1, 2 * CHUNK, S, 7)
         scatter(1, 2 * CHUNK, S)
         nc.sync.dma_start(out=out[P : 2 * P, :], in_=placed[1][:])

@@ -37,8 +37,7 @@ def tile_picked_route2_mlprelu_p_kernel(tc, x_words, x_scales, gate, w1, w2_word
         dst_sb = keep.tile([P, S // LANES], U16, name="dst_sb")
         x_win = [keep.tile([P, T], I32, name="x_win%d" % g, align_bytes=64) for g in range(PASSES)]
         xs_win = keep.tile([P, T], U8, name="xs_win", align_bytes=64)
-        x_pick = [keep.tile([P, S - g * CHUNK], U32, name="x_pick%d" % g, align_bytes=64) for g in range(PASSES)]
-        bias0 = keep.tile([P, 1], F32, name="bias0", tag="late", align_bytes=64)
+        x_pick = [keep.tile([P, S], U32, name="x_pick%d" % g, align_bytes=64) for g in range(PASSES)]
         xs_pick = keep.tile([P, S], U8, name="xs_pick", align_bytes=64)
         w1_raw = [
             keep.tile([P, PACK, H], F32, name="w1_raw%d" % g, tag="stage%d" % g, align_bytes=64)
@@ -60,7 +59,6 @@ def tile_picked_route2_mlprelu_p_kernel(tc, x_words, x_scales, gate, w1, w2_word
         banks = [psum.tile([P, PACK * TILE], F32, name="bank%d" % i) for i in range(S // TILE)]
 
         nc.vector.memset(zero[:], 0.0)
-        nc.vector.memset(bias0[:], 0.0)
         nc.vector.memset(xs_win[:].bitcast(I32), 0)
         nc.vector.memset(w2_sc[:].bitcast(I32), 0)
         nc.scalar.activation(out=placed[0][:], in_=zero[:, 0:1].to_broadcast([P, U]), func=RELU)
@@ -102,8 +100,6 @@ def tile_picked_route2_mlprelu_p_kernel(tc, x_words, x_scales, gate, w1, w2_word
             return tile[:, a // LANES : b // LANES]
 
         def picked(g, a, b):
-            if g == 1 and a >= S - CHUNK:
-                return x_pick[2][:, a - (S - CHUNK) : b - (S - CHUNK)]
             return x_pick[g][:, a:b]
 
         def h_values(a, b):
@@ -155,7 +151,7 @@ def tile_picked_route2_mlprelu_p_kernel(tc, x_words, x_scales, gate, w1, w2_word
             for t in range(PACK):
                 h_pass(i, t, 0)
 
-        def h_tile(i, bias=0.0):
+        def h_tile(i):
             if i >= OPENED:
                 open_tile(i)
             for t in range(PACK):
@@ -164,7 +160,6 @@ def tile_picked_route2_mlprelu_p_kernel(tc, x_words, x_scales, gate, w1, w2_word
                 out=h_values(i * TILE, (i + 1) * TILE).rearrange("p (n t) -> p n t", t=PACK),
                 in_=banks[H_BANK[i]][:].rearrange("p (t n) -> p n t", t=PACK),
                 func=RELU,
-                bias=bias,
             )
 
         def quantize_h(a, b):
@@ -216,12 +211,10 @@ def tile_picked_route2_mlprelu_p_kernel(tc, x_words, x_scales, gate, w1, w2_word
         warm(w1_codes[1][:, :P], w1_sc[1][:, :P])
         gather_words(1, 0, CHUNK)
         gather_words(1, CHUNK, 2 * CHUNK)
-        gather_words(1, 2 * CHUNK, 3 * CHUNK)
+        gather_words(1, 2 * CHUNK, S)
 
-        h_tile(0, bias0[:])
+        h_tile(0)
         quantize_h(0, TILE)
-        x_pick.append(keep.tile([P, CHUNK], U32, name="x_pick2", tag="late", align_bytes=64))
-        gather_words(1, 3 * CHUNK, S)
         y_pass(0, 0, TILE, 4, 0)
         h_tile(1)
         quantize_h(TILE, CHUNK)

@@ -157,8 +157,8 @@ def tile_picked_route2_mlprelu_p_kernel(tc, x_words, x_scales, gate, w1, w2_word
             for t in range(PACK):
                 h_pass(i, t, 1)
             nc.scalar.activation(
-                out=h_values(i * TILE, (i + 1) * TILE).rearrange("p (n t) -> p n t", t=PACK),
-                in_=banks[H_BANK[i]][:].rearrange("p (t n) -> p n t", t=PACK),
+                out=h_values(i * TILE, (i + 1) * TILE).rearrange("p (c i t) -> p c t i", i=2, t=PACK),
+                in_=banks[H_BANK[i]][:].rearrange("p (t c i) -> p c t i", i=2, t=PACK),
                 func=RELU,
             )
 

@@ -13,8 +13,8 @@ U16 = mybir.dt.uint16
 U8 = mybir.dt.uint8
 FP8X4 = mybir.dt.float8_e4m3fn_x4
 RELU = mybir.ActivationFunctionType.Relu
+COPY = mybir.ActivationFunctionType.Copy
 MULT = mybir.AluOpType.mult
-ADD = mybir.AluOpType.add
 
 P = 128
 PACK = 4
@@ -22,9 +22,8 @@ PASSES = K // (P * PACK)
 TILE = 128
 CHUNK = 256
 LANES = 16
-OPENED = 4
-H_BANK = (0, 1, 2, 3, 4, 5, 3, 0)
 SHARE = (48, 64)
+H_PIECES = ((0, 128), (128, 256), (256, 384), (384, 512), (512, 768), (768, 1024))
 
 
 def tile_picked_route2_mlprelu_p_kernel(tc, x_words, x_scales, gate, w1, w2_words, w2_scales, offs, dst, out):
@@ -36,26 +35,30 @@ def tile_picked_route2_mlprelu_p_kernel(tc, x_words, x_scales, gate, w1, w2_word
         offs_sb = keep.tile([P, S // LANES], U16, name="offs_sb")
         dst_sb = keep.tile([P, S // LANES], U16, name="dst_sb")
         x_win = [keep.tile([P, T], I32, name="x_win%d" % g, align_bytes=64) for g in range(PASSES)]
+        xs_rows = keep.tile([P, T // 4], I32, name="xs_rows", align_bytes=64)
         xs_win = keep.tile([P, T], U8, name="xs_win", align_bytes=64)
-        x_pick = [keep.tile([P, S], U32, name="x_pick%d" % g, align_bytes=64) for g in range(PASSES)]
+        x_pick = [keep.tile([P, S - g * CHUNK], U32, name="x_pick%d" % g, align_bytes=64) for g in range(PASSES)]
         xs_pick = keep.tile([P, S], U8, name="xs_pick", align_bytes=64)
         w1_raw = [
             keep.tile([P, PACK, H], F32, name="w1_raw%d" % g, tag="stage%d" % g, align_bytes=64)
             for g in range(PASSES)
         ]
-        xs_rows = keep.tile([P, T // 4], I32, name="xs_rows", align_bytes=64)
         w1_bf = [keep.tile([P, PACK * H], BF16, name="w1_bf%d" % g, align_bytes=64) for g in range(PASSES)]
         w1_codes = [keep.tile([P, H], U32, name="w1_codes%d" % g, align_bytes=64) for g in range(PASSES)]
         w1_sc = [keep.tile([P, H], U8, name="w1_sc%d" % g, align_bytes=64) for g in range(PASSES)]
         w2_codes = keep.tile([P, N], I32, name="w2_codes", align_bytes=64)
         w2_sc = keep.tile([P, N], U8, name="w2_sc", align_bytes=64)
         gate_sb = keep.tile([P, S], F32, name="gate_sb", align_bytes=64)
-        h_bf = keep.tile([P, PACK * S], BF16, name="h_bf", align_bytes=64)
+        h_bf = [
+            keep.tile([P, PACK * (b - a)], BF16, name="h_bf%d" % a, tag="h_bf%d" % a, align_bytes=64)
+            for a, b in H_PIECES
+        ]
         h_codes = keep.tile([P, S], U32, name="h_codes", align_bytes=64)
         h_sc = keep.tile([P, S], U8, name="h_sc", align_bytes=64)
-        y_sb = [keep.tile([P, S], F32, name="y_sb%d" % b, align_bytes=64) for b in range(N // P)]
+        y_plain = keep.tile([P, S], F32, name="y_plain", align_bytes=64)
+        y_gated = keep.tile([P, S], F32, name="y_gated", align_bytes=64)
         placed = [keep.tile([P, U], F32, name="placed0", align_bytes=64)]
-        zero = keep.tile([P, TILE], F32, name="zero", align_bytes=64)
+        zero = keep.tile([P, 8], F32, name="zero", align_bytes=64)
         banks = [psum.tile([P, PACK * TILE], F32, name="bank%d" % i) for i in range(S // TILE)]
 
         nc.vector.memset(zero[:], 0.0)
@@ -92,73 +95,55 @@ def tile_picked_route2_mlprelu_p_kernel(tc, x_words, x_scales, gate, w1, w2_word
             )
         load_x(1)
         nc.sync.dma_start(out=w2_codes[:], in_=w2_words[0].rearrange("p n t -> p (n t)").bitcast(I32))
-        nc.sync.dma_start(out=gate_sb[:, :TILE], in_=gate[:, :TILE])
+        nc.sync.dma_start(out=gate_sb[:, :CHUNK], in_=gate[:, :CHUNK])
         nc.sync.dma_start(dst_sb[:], dst)
-        nc.sync.dma_start(out=gate_sb[:, TILE:], in_=gate[:, TILE:])
+        nc.sync.dma_start(out=gate_sb[:, CHUNK:], in_=gate[:, CHUNK:])
 
         def entries(tile, a, b):
             return tile[:, a // LANES : b // LANES]
 
         def picked(g, a, b):
+            if g == 1 and a >= S - CHUNK:
+                return x_pick[2][:, a - S + CHUNK : b - S + CHUNK]
             return x_pick[g][:, a:b]
 
         def h_values(a, b):
-            return h_bf[:, PACK * a : PACK * b]
-
-        def warm(codes, scales):
-            nc.tensor.matmul_mx(
-                out=banks[7][:],
-                lhsT=codes.bitcast(FP8X4),
-                lhsT_scale=scales,
-                rhs=w1_codes[0][:].bitcast(FP8X4),
-                rhs_scale=w1_sc[0][:],
-                start=True,
-                stop=True,
-            )
+            n = [lo <= a < hi for lo, hi in H_PIECES].index(True)
+            lo = H_PIECES[n][0]
+            return h_bf[n][:, PACK * (a - lo) : PACK * (b - lo)]
 
         def gather_words(g, a, b):
             nc.vector.tensor_copy(
                 out=picked(g, a, b), in_=x_win[g][:].bitcast(U32).indirect(entries(offs_sb, a, b))
             )
 
-        def weave_views(g, a, b):
-            return (
-                w1_bf[g][:].rearrange("p (t m j) -> p m j t", t=PACK, j=PACK)[:, a:b],
-                w1_raw[g][:].rearrange("p j (m t) -> p m j t", t=PACK)[:, a:b],
-            )
-
         def weave(g, a, b, copy):
-            o, i = weave_views(g, a, b)
-            copy(out=o, in_=i)
+            copy(
+                out=w1_bf[g][:].rearrange("p (t m j) -> p m j t", t=PACK, j=PACK)[:, a:b],
+                in_=w1_raw[g][:].rearrange("p j (m t) -> p m j t", t=PACK)[:, a:b],
+            )
 
         def quantize_w1(g):
             nc.vector.quantize_mx(out=w1_codes[g][:].bitcast(FP8X4), scales=w1_sc[g][:], in_=w1_bf[g][:])
 
-        def h_pass(i, t, g):
+        def h_passes(i, g):
             cols = slice(i * TILE, (i + 1) * TILE)
-            chans = slice(t * P, (t + 1) * P)
-            nc.tensor.matmul_mx(
-                out=banks[H_BANK[i]][:, t * TILE : (t + 1) * TILE],
-                lhsT=w1_codes[g][:, chans].bitcast(FP8X4),
-                lhsT_scale=w1_sc[g][:, chans],
-                rhs=picked(g, i * TILE, (i + 1) * TILE).bitcast(FP8X4),
-                rhs_scale=xs_pick[4 * g :, cols],
-                start=(g == 0 and t == 0),
-                stop=(g == PASSES - 1 and t == PACK - 1),
-            )
-
-        def open_tile(i):
             for t in range(PACK):
-                h_pass(i, t, 0)
+                chans = slice(t * P, (t + 1) * P)
+                nc.tensor.matmul_mx(
+                    out=banks[i][:, t * TILE : (t + 1) * TILE],
+                    lhsT=w1_codes[g][:, chans].bitcast(FP8X4),
+                    lhsT_scale=w1_sc[g][:, chans],
+                    rhs=picked(g, i * TILE, (i + 1) * TILE).bitcast(FP8X4),
+                    rhs_scale=xs_pick[4 * g :, cols],
+                    start=(g == 0 and t == 0),
+                    stop=(g == PASSES - 1 and t == PACK - 1),
+                )
 
-        def h_tile(i):
-            if i >= OPENED:
-                open_tile(i)
-            for t in range(PACK):
-                h_pass(i, t, 1)
+        def relu(i):
             nc.scalar.activation(
                 out=h_values(i * TILE, (i + 1) * TILE).rearrange("p (c i t) -> p c t i", i=2, t=PACK),
-                in_=banks[H_BANK[i]][:].rearrange("p (t c i) -> p c t i", i=2, t=PACK),
+                in_=banks[i][:].rearrange("p (t c i) -> p c t i", i=2, t=PACK),
                 func=RELU,
             )
 
@@ -167,25 +152,36 @@ def tile_picked_route2_mlprelu_p_kernel(tc, x_words, x_scales, gate, w1, w2_word
                 out=h_codes[:, a:b].bitcast(FP8X4), scales=h_sc[:, a:b], in_=h_values(a, b)
             )
 
-        def y_pass(b, a, e, bank, at):
+        def y_pass(b, c, bank):
             rows = slice(b * P, (b + 1) * P)
+            cols = slice(c * CHUNK, (c + 1) * CHUNK)
             nc.tensor.matmul_mx(
-                out=banks[bank][:, at : at + e - a],
+                out=banks[bank][:, :CHUNK],
                 lhsT=w2_codes[:, rows].bitcast(FP8X4),
                 lhsT_scale=w2_sc[:, rows],
-                rhs=h_codes[:, a:e].bitcast(FP8X4),
-                rhs_scale=h_sc[:, a:e],
+                rhs=h_codes[:, cols].bitcast(FP8X4),
+                rhs_scale=h_sc[:, cols],
                 start=True,
                 stop=True,
             )
 
-        def y_copy(b, a, e, bank):
-            nc.scalar.copy(out=y_sb[b][:, a:e], in_=banks[bank][:, : e - a])
+        def copy_y0(c, bank):
+            y_pass(0, c, bank)
+            nc.scalar.copy(out=y_plain[:, c * CHUNK : (c + 1) * CHUNK], in_=banks[bank][:, :CHUNK])
 
-        def scatter(b, a, e):
+        def gate_y1(c, bank):
+            cols = slice(c * CHUNK, (c + 1) * CHUNK)
+            y_pass(1, c, bank)
+            nc.vector.tensor_tensor(y_gated[:, cols], banks[bank][:, :CHUNK], gate_sb[:, cols], MULT)
+
+        def scatter0(c):
+            a, e = c * CHUNK, (c + 1) * CHUNK
             nc.vector.tensor_tensor(
-                placed[b][:].indirect(entries(dst_sb, a, e)), y_sb[b][:, a:e], gate_sb[:, a:e], MULT
+                placed[0][:].indirect(entries(dst_sb, a, e)), y_plain[:, a:e], gate_sb[:, a:e], MULT
             )
+
+        def scatter1(a, e):
+            nc.scalar.activation(out=placed[1][:].indirect(entries(dst_sb, a, e)), in_=y_gated[:, a:e], func=COPY)
 
         for q in range(4):
             live = slice(32 * q, 32 * q + 4 * PASSES)
@@ -196,55 +192,49 @@ def tile_picked_route2_mlprelu_p_kernel(tc, x_words, x_scales, gate, w1, w2_word
         placed.append(keep.tile([P, U], F32, name="placed1", tag="stage0", align_bytes=64))
         nc.scalar.activation(out=placed[1][:], in_=zero[:, 0:1].to_broadcast([P, U]), func=RELU)
         quantize_w1(0)
-        warm(w1_codes[0][:, :P], w1_sc[0][:, :P])
-        for a in (0, CHUNK):
-            gather_words(0, a, a + CHUNK)
-            for i in range(a // TILE, (a + CHUNK) // TILE):
-                open_tile(i)
-        gather_words(0, S // 2, S)
-        warm(x_pick[0][:, S - P :], xs_pick[:, S - P :])
-        warm(x_pick[0][:, S - P :], xs_pick[:, S - P :])
+        for a, b in ((0, CHUNK), (CHUNK, 2 * CHUNK), (2 * CHUNK, S)):
+            gather_words(0, a, b)
+        for i in range(S // TILE):
+            h_passes(i, 0)
         weave(1, 0, SHARE[1], nc.vector.tensor_copy)
         weave(1, SHARE[1], P, nc.scalar.copy)
         quantize_w1(1)
-        warm(w1_codes[1][:, :P], w1_sc[1][:, :P])
-        warm(w1_codes[1][:, :P], w1_sc[1][:, :P])
-        gather_words(1, 0, CHUNK)
-        gather_words(1, CHUNK, 2 * CHUNK)
-        gather_words(1, 2 * CHUNK, S)
+        for a, b in ((0, TILE), (TILE, CHUNK), (CHUNK, 2 * CHUNK), (2 * CHUNK, 3 * CHUNK)):
+            gather_words(1, a, b)
+            for i in range(a // TILE, b // TILE):
+                h_passes(i, 1)
 
-        h_tile(0)
-        quantize_h(0, TILE)
-        y_pass(0, 0, TILE, 4, 0)
-        h_tile(1)
-        quantize_h(TILE, CHUNK)
-        y_pass(1, 0, CHUNK, 5, 0)
-        first = keep.tile([P, TILE], F32, name="first", align_bytes=64)
-        nc.vector.tensor_tensor(first[:], banks[4][:, :TILE], gate_sb[:, :TILE], MULT)
-        h_tile(2)
-        quantize_h(CHUNK, 3 * TILE)
-        nc.vector.tensor_tensor(placed[0][:].indirect(entries(dst_sb, 0, TILE)), first[:], zero[:], ADD)
-        h_tile(3)
-        quantize_h(3 * TILE, 2 * CHUNK)
-        y_copy(1, 0, CHUNK, 5)
-        scatter(1, 0, CHUNK)
-        y_pass(0, TILE, CHUNK, 0, 0)
-        y_pass(0, CHUNK, 2 * CHUNK, 0, TILE)
-        y_copy(0, TILE, 2 * CHUNK, 0)
-        scatter(0, TILE, 2 * CHUNK)
-        for i in range(4, 8):
-            h_tile(i)
-        quantize_h(2 * CHUNK, S)
-        y_pass(1, CHUNK, 2 * CHUNK, 0, 0)
-        y_copy(1, CHUNK, 2 * CHUNK, 0)
-        scatter(1, CHUNK, 2 * CHUNK)
-        y_pass(0, 2 * CHUNK, 3 * CHUNK, 6, 0)
-        y_copy(0, 2 * CHUNK, 3 * CHUNK, 6)
-        y_pass(0, 3 * CHUNK, S, 1, 0)
-        y_copy(0, 3 * CHUNK, S, 1)
-        scatter(0, 2 * CHUNK, S)
+        for i in range(2):
+            relu(i)
+            quantize_h(i * TILE, (i + 1) * TILE)
+        x_pick.append(keep.tile([P, CHUNK], U32, name="x_pick_last", tag="h_bf128", align_bytes=64))
+        gather_words(1, 3 * CHUNK, S)
+        relu(2)
+        quantize_h(2 * TILE, 3 * TILE)
+        copy_y0(0, 0)
+        gate_y1(0, 1)
+        for i in range(6, 8):
+            h_passes(i, 1)
+        scatter0(0)
+        relu(3)
+        quantize_h(3 * TILE, 4 * TILE)
+        relu(4)
+        relu(5)
+        quantize_h(2 * CHUNK, 3 * CHUNK)
+        gate_y1(1, 2)
+        relu(6)
+        copy_y0(1, 5)
+        scatter0(1)
+        relu(7)
+        quantize_h(3 * CHUNK, S)
+        copy_y0(2, 0)
+        gate_y1(2, 7)
+        scatter0(2)
+        scatter1(0, 3 * TILE)
+        copy_y0(3, 6)
+        scatter0(3)
         nc.sync.dma_start(out=out[0:P, :], in_=placed[0][:])
-        y_pass(1, 2 * CHUNK, S, 7, 0)
-        y_copy(1, 2 * CHUNK, S, 7)
-        scatter(1, 2 * CHUNK, S)
+        scatter1(3 * TILE, 6 * TILE)
+        gate_y1(3, 6)
+        scatter1(6 * TILE, S)
         nc.sync.dma_start(out=out[P : 2 * P, :], in_=placed[1][:])

@@ -23,7 +23,10 @@ TILE = 128
 CHUNK = 256
 LANES = 16
 SHARE = (48, 64)
-H_PIECES = ((0, 128), (128, 256), (256, 384), (384, 512), (512, 768), (768, 1024))
+H_PIECES = ((0, 128), (128, 256), (256, 512), (512, 768), (768, 1024))
+HELD = 256
+OPENED = 6
+H_BANK = (0, 1, 2, 3, 4, 5, 7, 6)
 
 
 def tile_picked_route2_mlprelu_p_kernel(tc, x_words, x_scales, gate, w1, w2_words, w2_scales, offs, dst, out):
@@ -37,7 +40,7 @@ def tile_picked_route2_mlprelu_p_kernel(tc, x_words, x_scales, gate, w1, w2_word
         x_win = [keep.tile([P, T], I32, name="x_win%d" % g, align_bytes=64) for g in range(PASSES)]
         xs_rows = keep.tile([P, T // 4], I32, name="xs_rows", align_bytes=64)
         xs_win = keep.tile([P, T], U8, name="xs_win", align_bytes=64)
-        x_pick = [keep.tile([P, S - g * CHUNK], U32, name="x_pick%d" % g, align_bytes=64) for g in range(PASSES)]
+        x_pick = [keep.tile([P, S - g * HELD], U32, name="x_pick%d" % g, align_bytes=64) for g in range(PASSES)]
         xs_pick = keep.tile([P, S], U8, name="xs_pick", align_bytes=64)
         w1_raw = [
             keep.tile([P, PACK, H], F32, name="w1_raw%d" % g, tag="stage%d" % g, align_bytes=64)
@@ -103,8 +106,8 @@ def tile_picked_route2_mlprelu_p_kernel(tc, x_words, x_scales, gate, w1, w2_word
             return tile[:, a // LANES : b // LANES]
 
         def picked(g, a, b):
-            if g == 1 and a >= S - CHUNK:
-                return x_pick[2][:, a - S + CHUNK : b - S + CHUNK]
+            if g == 1 and a >= S - HELD:
+                return x_pick[2][:, a - S + HELD : b - S + HELD]
             return x_pick[g][:, a:b]
 
         def h_values(a, b):
@@ -131,7 +134,7 @@ def tile_picked_route2_mlprelu_p_kernel(tc, x_words, x_scales, gate, w1, w2_word
             for t in range(PACK):
                 chans = slice(t * P, (t + 1) * P)
                 nc.tensor.matmul_mx(
-                    out=banks[i][:, t * TILE : (t + 1) * TILE],
+                    out=banks[H_BANK[i]][:, t * TILE : (t + 1) * TILE],
                     lhsT=w1_codes[g][:, chans].bitcast(FP8X4),
                     lhsT_scale=w1_sc[g][:, chans],
                     rhs=picked(g, i * TILE, (i + 1) * TILE).bitcast(FP8X4),
@@ -143,7 +146,7 @@ def tile_picked_route2_mlprelu_p_kernel(tc, x_words, x_scales, gate, w1, w2_word
         def relu(i):
             nc.scalar.activation(
                 out=h_values(i * TILE, (i + 1) * TILE).rearrange("p (c i t) -> p c t i", i=2, t=PACK),
-                in_=banks[i][:].rearrange("p (t c i) -> p c t i", i=2, t=PACK),
+                in_=banks[H_BANK[i]][:].rearrange("p (t c i) -> p c t i", i=2, t=PACK),
                 func=RELU,
             )
 
@@ -152,11 +155,11 @@ def tile_picked_route2_mlprelu_p_kernel(tc, x_words, x_scales, gate, w1, w2_word
                 out=h_codes[:, a:b].bitcast(FP8X4), scales=h_sc[:, a:b], in_=h_values(a, b)
             )
 
-        def y_pass(b, c, bank):
+        def y_pass(b, c, bank, at=0):
             rows = slice(b * P, (b + 1) * P)
             cols = slice(c * CHUNK, (c + 1) * CHUNK)
             nc.tensor.matmul_mx(
-                out=banks[bank][:, :CHUNK],
+                out=banks[bank][:, at : at + CHUNK],
                 lhsT=w2_codes[:, rows].bitcast(FP8X4),
                 lhsT_scale=w2_sc[:, rows],
                 rhs=h_codes[:, cols].bitcast(FP8X4),
@@ -166,13 +169,11 @@ def tile_picked_route2_mlprelu_p_kernel(tc, x_words, x_scales, gate, w1, w2_word
             )
 
         def copy_y0(c, bank):
-            y_pass(0, c, bank)
             nc.scalar.copy(out=y_plain[:, c * CHUNK : (c + 1) * CHUNK], in_=banks[bank][:, :CHUNK])
 
-        def gate_y1(c, bank):
+        def gate_y1(c, bank, at=0):
             cols = slice(c * CHUNK, (c + 1) * CHUNK)
-            y_pass(1, c, bank)
-            nc.vector.tensor_tensor(y_gated[:, cols], banks[bank][:, :CHUNK], gate_sb[:, cols], MULT)
+            nc.vector.tensor_tensor(y_gated[:, cols], banks[bank][:, at : at + CHUNK], gate_sb[:, cols], MULT)
 
         def scatter0(c):
             a, e = c * CHUNK, (c + 1) * CHUNK
@@ -192,14 +193,14 @@ def tile_picked_route2_mlprelu_p_kernel(tc, x_words, x_scales, gate, w1, w2_word
         placed.append(keep.tile([P, U], F32, name="placed1", tag="stage0", align_bytes=64))
         nc.scalar.activation(out=placed[1][:], in_=zero[:, 0:1].to_broadcast([P, U]), func=RELU)
         quantize_w1(0)
-        for a, b in ((0, CHUNK), (CHUNK, 2 * CHUNK), (2 * CHUNK, S)):
+        for a, b in ((0, TILE), (TILE, 3 * TILE), (3 * TILE, 3 * CHUNK), (3 * CHUNK, S)):
             gather_words(0, a, b)
-        for i in range(S // TILE):
+        for i in range(OPENED):
             h_passes(i, 0)
         weave(1, 0, SHARE[1], nc.vector.tensor_copy)
         weave(1, SHARE[1], P, nc.scalar.copy)
         quantize_w1(1)
-        for a, b in ((0, TILE), (TILE, CHUNK), (CHUNK, 2 * CHUNK), (2 * CHUNK, 3 * CHUNK)):
+        for a, b in ((0, TILE), (TILE, CHUNK), (CHUNK, 2 * CHUNK), (2 * CHUNK, S - HELD)):
             gather_words(1, a, b)
             for i in range(a // TILE, b // TILE):
                 h_passes(i, 1)
@@ -207,34 +208,42 @@ def tile_picked_route2_mlprelu_p_kernel(tc, x_words, x_scales, gate, w1, w2_word
         for i in range(2):
             relu(i)
             quantize_h(i * TILE, (i + 1) * TILE)
-        x_pick.append(keep.tile([P, CHUNK], U32, name="x_pick_last", tag="h_bf128", align_bytes=64))
-        gather_words(1, 3 * CHUNK, S)
+        x_pick.append(keep.tile([P, HELD], U32, name="x_pick_last", tag="h_bf128", align_bytes=64))
+        gather_words(1, S - HELD, S)
         relu(2)
-        quantize_h(2 * TILE, 3 * TILE)
-        copy_y0(0, 0)
-        gate_y1(0, 1)
-        for i in range(6, 8):
-            h_passes(i, 1)
-        scatter0(0)
         relu(3)
-        quantize_h(3 * TILE, 4 * TILE)
+        y_pass(0, 0, 6)
+        copy_y0(0, 6)
+        y_pass(1, 0, 7)
+        gate_y1(0, 7)
+        quantize_h(CHUNK, 2 * CHUNK)
+        scatter0(0)
         relu(4)
         relu(5)
         quantize_h(2 * CHUNK, 3 * CHUNK)
-        gate_y1(1, 2)
-        relu(6)
-        copy_y0(1, 5)
+        y_pass(0, 1, 4)
+        y_pass(1, 1, 4, CHUNK)
+        for i in range(OPENED, S // TILE):
+            h_passes(i, 0)
+            h_passes(i, 1)
+        copy_y0(1, 4)
+        gate_y1(1, 4, CHUNK)
         scatter0(1)
+        relu(6)
         relu(7)
         quantize_h(3 * CHUNK, S)
+        y_pass(0, 2, 0)
         copy_y0(2, 0)
-        gate_y1(2, 7)
+        y_pass(1, 2, 6)
+        gate_y1(2, 6)
         scatter0(2)
         scatter1(0, 3 * TILE)
-        copy_y0(3, 6)
+        y_pass(0, 3, 7)
+        copy_y0(3, 7)
         scatter0(3)
         nc.sync.dma_start(out=out[0:P, :], in_=placed[0][:])
         scatter1(3 * TILE, 6 * TILE)
-        gate_y1(3, 6)
+        y_pass(1, 3, 7)
+        gate_y1(3, 7)
         scatter1(6 * TILE, S)
         nc.sync.dma_start(out=out[P : 2 * P, :], in_=placed[1][:])

@@ -240,10 +240,10 @@ def tile_picked_route2_mlprelu_p_kernel(tc, x_words, x_scales, gate, w1, w2_word
         scatter1(0, 3 * TILE)
         y_pass(0, 3, 7)
         copy_y0(3, 7)
+        y_pass(1, 3, 1)
+        gate_y1(3, 1)
         scatter0(3)
         nc.sync.dma_start(out=out[0:P, :], in_=placed[0][:])
         scatter1(3 * TILE, 6 * TILE)
-        y_pass(1, 3, 7)
-        gate_y1(3, 7)
         scatter1(6 * TILE, S)
         nc.sync.dma_start(out=out[P : 2 * P, :], in_=placed[1][:])

@@ -61,13 +61,13 @@ def tile_picked_route2_mlprelu_p_kernel(tc, x_words, x_scales, gate, w1, w2_word
         y_plain = keep.tile([P, S], F32, name="y_plain", align_bytes=64)
         y_gated = keep.tile([P, S], F32, name="y_gated", align_bytes=64)
         placed = [keep.tile([P, U], F32, name="placed0", align_bytes=64)]
-        zero = keep.tile([P, 8], F32, name="zero", align_bytes=64)
+        zero = keep.tile([P, 1], F32, name="zero", align_bytes=64)
         banks = [psum.tile([P, PACK * TILE], F32, name="bank%d" % i) for i in range(S // TILE)]
 
         nc.vector.memset(zero[:], 0.0)
         nc.vector.memset(xs_win[:].bitcast(I32), 0)
         nc.vector.memset(w2_sc[:].bitcast(I32), 0)
-        nc.scalar.activation(out=placed[0][:], in_=zero[:, 0:1].to_broadcast([P, U]), func=RELU)
+        nc.scalar.activation(out=placed[0][:], in_=zero[:].to_broadcast([P, U]), func=RELU)
 
         def load_w1(g):
             rows = w1[g * P * PACK : (g + 1) * P * PACK, :]
@@ -191,7 +191,7 @@ def tile_picked_route2_mlprelu_p_kernel(tc, x_words, x_scales, gate, w1, w2_word
         weave(0, 0, SHARE[0], nc.vector.tensor_copy)
         weave(0, SHARE[0], P, nc.scalar.copy)
         placed.append(keep.tile([P, U], F32, name="placed1", tag="stage0", align_bytes=64))
-        nc.scalar.activation(out=placed[1][:], in_=zero[:, 0:1].to_broadcast([P, U]), func=RELU)
+        nc.scalar.activation(out=placed[1][:], in_=zero[:].to_broadcast([P, U]), func=RELU)
         quantize_w1(0)
         for a, b in ((0, TILE), (TILE, 3 * TILE), (3 * TILE, 3 * CHUNK), (3 * CHUNK, S)):
             gather_words(0, a, b)
@@ -246,4 +246,4 @@ def tile_picked_route2_mlprelu_p_kernel(tc, x_words, x_scales, gate, w1, w2_word
         nc.sync.dma_start(out=out[0:P, :], in_=placed[0][:])
         scatter1(3 * TILE, 6 * TILE)
         scatter1(6 * TILE, S)
-        nc.sync.dma_start(out=out[P : 2 * P, :], in_=placed[1][:])
+        nc.scalar.dma_start(out=out[P : 2 * P, :], in_=placed[1][:])

@@ -54,9 +54,12 @@ def tile_picked_route2_mlprelu_p_kernel(tc, x_words, x_scales, gate, w1, w2_word
         gate_sb = keep.tile([P, S], F32, name="gate_sb", align_bytes=64)
         h_bf = [
             keep.tile([P, PACK * (b - a)], BF16, name="h_bf%d" % a, tag="h_bf%d" % a, align_bytes=64)
-            for a, b in H_PIECES
+            for a, b in H_PIECES[:3]
         ]
-        h_codes = keep.tile([P, S], U32, name="h_codes", align_bytes=64)
+        h_codes = [
+            keep.tile([P, CHUNK], U32, name="h_codes%d" % c, tag="h_codes%d" % c, align_bytes=64)
+            for c in range(S // CHUNK)
+        ]
         h_sc = keep.tile([P, S], U8, name="h_sc", align_bytes=64)
         y_plain = keep.tile([P, S], F32, name="y_plain", align_bytes=64)
         y_gated = keep.tile([P, S], F32, name="y_gated", align_bytes=64)
@@ -91,13 +94,13 @@ def tile_picked_route2_mlprelu_p_kernel(tc, x_words, x_scales, gate, w1, w2_word
         load_w1(0)
         load_x(0)
         load_w1(1)
+        load_x(1)
+        nc.sync.dma_start(out=w2_codes[:], in_=w2_words[0].rearrange("p n t -> p (n t)").bitcast(I32))
         for q in range(4):
             nc.sync.dma_start(
                 out=w2_sc[32 * q : 32 * q + 4, :].bitcast(I32),
                 in_=w2_scales[0, 4 * q : 4 * q + 4, :].bitcast(I32),
             )
-        load_x(1)
-        nc.sync.dma_start(out=w2_codes[:], in_=w2_words[0].rearrange("p n t -> p (n t)").bitcast(I32))
         nc.sync.dma_start(out=gate_sb[:, :CHUNK], in_=gate[:, :CHUNK])
         nc.sync.dma_start(dst_sb[:], dst)
         nc.sync.dma_start(out=gate_sb[:, CHUNK:], in_=gate[:, CHUNK:])
@@ -152,7 +155,7 @@ def tile_picked_route2_mlprelu_p_kernel(tc, x_words, x_scales, gate, w1, w2_word
 
         def quantize_h(a, b):
             nc.vector.quantize_mx(
-                out=h_codes[:, a:b].bitcast(FP8X4), scales=h_sc[:, a:b], in_=h_values(a, b)
+                out=h_codes[a // CHUNK][:, a % CHUNK : a % CHUNK + b - a].bitcast(FP8X4), scales=h_sc[:, a:b], in_=h_values(a, b)
             )
 
         def y_pass(b, c, bank, at=0):
@@ -162,7 +165,7 @@ def tile_picked_route2_mlprelu_p_kernel(tc, x_words, x_scales, gate, w1, w2_word
                 out=banks[bank][:, at : at + CHUNK],
                 lhsT=w2_codes[:, rows].bitcast(FP8X4),
                 lhsT_scale=w2_sc[:, rows],
-                rhs=h_codes[:, cols].bitcast(FP8X4),
+                rhs=h_codes[c][:].bitcast(FP8X4),
                 rhs_scale=h_sc[:, cols],
                 start=True,
                 stop=True,
@@ -218,6 +221,8 @@ def tile_picked_route2_mlprelu_p_kernel(tc, x_words, x_scales, gate, w1, w2_word
         gate_y1(0, 7)
         quantize_h(CHUNK, 2 * CHUNK)
         scatter0(0)
+        h_bf.append(keep.tile([P, PACK * CHUNK], BF16, name="h_bf512", tag="h_codes0", align_bytes=64))
+        h_bf.append(keep.tile([P, PACK * CHUNK], BF16, name="h_bf768", align_bytes=64))
         relu(4)
         relu(5)
         quantize_h(2 * CHUNK, 3 * CHUNK)

@@ -60,7 +60,7 @@ def tile_picked_route2_mlprelu_p_kernel(tc, x_words, x_scales, gate, w1, w2_word
             keep.tile([P, CHUNK], U32, name="h_codes%d" % c, tag="h_codes%d" % c, align_bytes=64)
             for c in range(S // CHUNK)
         ]
-        h_sc = keep.tile([P, S], U8, name="h_sc", align_bytes=64)
+        h_sc = [keep.tile([P, CHUNK], U8, name="h_sc0", tag="h_sc01", align_bytes=64)]
         y_plain = keep.tile([P, S], F32, name="y_plain", align_bytes=64)
         y_gated = keep.tile([P, S], F32, name="y_gated", align_bytes=64)
         placed = [keep.tile([P, U], F32, name="placed0", align_bytes=64)]
@@ -96,12 +96,12 @@ def tile_picked_route2_mlprelu_p_kernel(tc, x_words, x_scales, gate, w1, w2_word
         load_w1(1)
         load_x(1)
         nc.sync.dma_start(out=w2_codes[:], in_=w2_words[0].rearrange("p n t -> p (n t)").bitcast(I32))
+        nc.sync.dma_start(out=gate_sb[:, :CHUNK], in_=gate[:, :CHUNK])
         for q in range(4):
             nc.sync.dma_start(
                 out=w2_sc[32 * q : 32 * q + 4, :].bitcast(I32),
                 in_=w2_scales[0, 4 * q : 4 * q + 4, :].bitcast(I32),
             )
-        nc.sync.dma_start(out=gate_sb[:, :CHUNK], in_=gate[:, :CHUNK])
         nc.sync.dma_start(dst_sb[:], dst)
         nc.sync.dma_start(out=gate_sb[:, CHUNK:], in_=gate[:, CHUNK:])
 
@@ -155,18 +155,17 @@ def tile_picked_route2_mlprelu_p_kernel(tc, x_words, x_scales, gate, w1, w2_word
 
         def quantize_h(a, b):
             nc.vector.quantize_mx(
-                out=h_codes[a // CHUNK][:, a % CHUNK : a % CHUNK + b - a].bitcast(FP8X4), scales=h_sc[:, a:b], in_=h_values(a, b)
+                out=h_codes[a // CHUNK][:, a % CHUNK : a % CHUNK + b - a].bitcast(FP8X4), scales=h_sc[a // CHUNK][:, a % CHUNK : a % CHUNK + b - a], in_=h_values(a, b)
             )
 
         def y_pass(b, c, bank, at=0):
             rows = slice(b * P, (b + 1) * P)
-            cols = slice(c * CHUNK, (c + 1) * CHUNK)
             nc.tensor.matmul_mx(
                 out=banks[bank][:, at : at + CHUNK],
                 lhsT=w2_codes[:, rows].bitcast(FP8X4),
                 lhsT_scale=w2_sc[:, rows],
                 rhs=h_codes[c][:].bitcast(FP8X4),
-                rhs_scale=h_sc[:, cols],
+                rhs_scale=h_sc[c][:],
                 start=True,
                 stop=True,
             )
@@ -219,6 +218,8 @@ def tile_picked_route2_mlprelu_p_kernel(tc, x_words, x_scales, gate, w1, w2_word
         copy_y0(0, 6)
         y_pass(1, 0, 7)
         gate_y1(0, 7)
+        h_sc.append(keep.tile([P, CHUNK], U8, name="h_sc1", tag="h_sc01", align_bytes=64))
+        h_sc.extend(keep.tile([P, CHUNK], U8, name="h_sc%d" % c, align_bytes=64) for c in (2, 3))
         quantize_h(CHUNK, 2 * CHUNK)
         scatter0(0)
         h_bf.append(keep.tile([P, PACK * CHUNK], BF16, name="h_bf512", tag="h_codes0", align_bytes=64))

@@ -25,7 +25,6 @@ LANES = 16
 SHARE = (48, 64)
 H_PIECES = ((0, 128), (128, 256), (256, 512), (512, 768), (768, 1024))
 HELD = 256
-OPENED = 6
 H_BANK = (0, 1, 2, 3, 4, 5, 7, 6)
 
 
@@ -94,14 +93,14 @@ def tile_picked_route2_mlprelu_p_kernel(tc, x_words, x_scales, gate, w1, w2_word
         load_w1(0)
         load_x(0)
         load_w1(1)
-        load_x(1)
-        nc.sync.dma_start(out=w2_codes[:], in_=w2_words[0].rearrange("p n t -> p (n t)").bitcast(I32))
-        nc.sync.dma_start(out=gate_sb[:, :CHUNK], in_=gate[:, :CHUNK])
         for q in range(4):
             nc.sync.dma_start(
                 out=w2_sc[32 * q : 32 * q + 4, :].bitcast(I32),
                 in_=w2_scales[0, 4 * q : 4 * q + 4, :].bitcast(I32),
             )
+        load_x(1)
+        nc.sync.dma_start(out=w2_codes[:], in_=w2_words[0].rearrange("p n t -> p (n t)").bitcast(I32))
+        nc.sync.dma_start(out=gate_sb[:, :CHUNK], in_=gate[:, :CHUNK])
         nc.sync.dma_start(dst_sb[:], dst)
         nc.sync.dma_start(out=gate_sb[:, CHUNK:], in_=gate[:, CHUNK:])
 
@@ -197,7 +196,7 @@ def tile_picked_route2_mlprelu_p_kernel(tc, x_words, x_scales, gate, w1, w2_word
         quantize_w1(0)
         for a, b in ((0, TILE), (TILE, 3 * TILE), (3 * TILE, 3 * CHUNK), (3 * CHUNK, S)):
             gather_words(0, a, b)
-        for i in range(OPENED):
+        for i in range(S // TILE):
             h_passes(i, 0)
         weave(1, 0, SHARE[1], nc.vector.tensor_copy)
         weave(1, SHARE[1], P, nc.scalar.copy)
@@ -214,27 +213,26 @@ def tile_picked_route2_mlprelu_p_kernel(tc, x_words, x_scales, gate, w1, w2_word
         gather_words(1, S - HELD, S)
         relu(2)
         relu(3)
-        y_pass(0, 0, 6)
-        copy_y0(0, 6)
-        y_pass(1, 0, 7)
-        gate_y1(0, 7)
+        y_pass(0, 0, 0)
+        copy_y0(0, 0)
+        y_pass(1, 0, 1)
+        gate_y1(0, 1)
         h_sc.append(keep.tile([P, CHUNK], U8, name="h_sc1", tag="h_sc01", align_bytes=64))
         h_sc.extend(keep.tile([P, CHUNK], U8, name="h_sc%d" % c, align_bytes=64) for c in (2, 3))
         quantize_h(CHUNK, 2 * CHUNK)
         scatter0(0)
         h_bf.append(keep.tile([P, PACK * CHUNK], BF16, name="h_bf512", tag="h_codes0", align_bytes=64))
-        h_bf.append(keep.tile([P, PACK * CHUNK], BF16, name="h_bf768", align_bytes=64))
         relu(4)
         relu(5)
         quantize_h(2 * CHUNK, 3 * CHUNK)
         y_pass(0, 1, 4)
         y_pass(1, 1, 4, CHUNK)
-        for i in range(OPENED, S // TILE):
-            h_passes(i, 0)
+        for i in range((S - HELD) // TILE, S // TILE):
             h_passes(i, 1)
         copy_y0(1, 4)
         gate_y1(1, 4, CHUNK)
         scatter0(1)
+        h_bf.append(keep.tile([P, PACK * CHUNK], BF16, name="h_bf768", tag="h_codes1", align_bytes=64))
         relu(6)
         relu(7)
         quantize_h(3 * CHUNK, S)

@@ -42,7 +42,7 @@ def tile_picked_route2_mlprelu_p_kernel(tc, x_words, x_scales, gate, w1, w2_word
         x_pick = [keep.tile([P, S - g * HELD], U32, name="x_pick%d" % g, align_bytes=64) for g in range(PASSES)]
         xs_pick = keep.tile([P, S], U8, name="xs_pick", align_bytes=64)
         w1_raw = [
-            keep.tile([P, PACK, H], F32, name="w1_raw%d" % g, tag="stage%d" % g, align_bytes=64)
+            keep.tile([P, PACK * H], F32, name="w1_raw%d" % g, tag="stage%d" % g, align_bytes=64)
             for g in range(PASSES)
         ]
         w1_bf = [keep.tile([P, PACK * H], BF16, name="w1_bf%d" % g, align_bytes=64) for g in range(PASSES)]
@@ -73,7 +73,7 @@ def tile_picked_route2_mlprelu_p_kernel(tc, x_words, x_scales, gate, w1, w2_word
 
         def load_w1(g):
             rows = w1[g * P * PACK : (g + 1) * P * PACK, :]
-            nc.sync.dma_start(out=w1_raw[g][:], in_=rows.rearrange("(p j) c -> p j c", j=PACK))
+            nc.sync.dma_start(out=w1_raw[g][:], in_=rows.rearrange("(p j) c -> p (j c)", j=PACK))
 
         def load_x(g):
             nc.sync.dma_start(out=x_win[g][:], in_=x_words[g].rearrange("p n t -> p (n t)").bitcast(I32))
@@ -125,7 +125,7 @@ def tile_picked_route2_mlprelu_p_kernel(tc, x_words, x_scales, gate, w1, w2_word
         def weave(g, a, b, copy):
             copy(
                 out=w1_bf[g][:].rearrange("p (t m j) -> p m j t", t=PACK, j=PACK)[:, a:b],
-                in_=w1_raw[g][:].rearrange("p j (m t) -> p m j t", t=PACK)[:, a:b],
+                in_=w1_raw[g][:].rearrange("p (j m t) -> p m j t", j=PACK, t=PACK)[:, a:b],
             )
 
         def quantize_w1(g):

@@ -32,13 +32,14 @@ def tile_picked_route2_mlprelu_p_kernel(tc, x_words, x_scales, gate, w1, w2_word
     nc = tc.nc
     with ExitStack() as ctx:
         keep = ctx.enter_context(tc.tile_pool(name="keep", bufs=1))
+        shared = ctx.enter_context(tc.tile_pool(name="shared", bufs=1))
         psum = ctx.enter_context(tc.psum_pool(name="psum", bufs=1))
 
         offs_sb = keep.tile([P, S // LANES], U16, name="offs_sb")
         dst_sb = keep.tile([P, S // LANES], U16, name="dst_sb")
         x_win = [keep.tile([P, T], I32, name="x_win%d" % g, align_bytes=64) for g in range(PASSES)]
         xs_rows = keep.tile([P, T // 4], I32, name="xs_rows", align_bytes=64)
-        xs_win = keep.tile([P, T], U8, name="xs_win", align_bytes=64)
+        xs_win = shared.tile([P, T], U8, name="xs_win", align_bytes=64, offset=0)
         x_pick = [keep.tile([P, S - g * HELD], U32, name="x_pick%d" % g, align_bytes=64) for g in range(PASSES)]
         xs_pick = keep.tile([P, S], U8, name="xs_pick", align_bytes=64)
         w1_raw = [
@@ -48,9 +49,8 @@ def tile_picked_route2_mlprelu_p_kernel(tc, x_words, x_scales, gate, w1, w2_word
         w1_bf = [keep.tile([P, PACK * H], BF16, name="w1_bf%d" % g, align_bytes=64) for g in range(PASSES)]
         w1_codes = [keep.tile([P, H], U32, name="w1_codes%d" % g, align_bytes=64) for g in range(PASSES)]
         w1_sc = [keep.tile([P, H], U8, name="w1_sc%d" % g, align_bytes=64) for g in range(PASSES)]
-        w2_codes = keep.tile([P, N], I32, name="w2_codes", align_bytes=64)
+        xs_last = keep.tile([P, S], U8, name="xs_last", align_bytes=64)
         w2_sc = keep.tile([P, N], U8, name="w2_sc", align_bytes=64)
-        gate_sb = keep.tile([P, S], F32, name="gate_sb", align_bytes=64)
         h_bf = [
             keep.tile([P, PACK * (b - a)], BF16, name="h_bf%d" % a, tag="h_bf%d" % a, align_bytes=64)
             for a, b in H_PIECES[:3]
@@ -69,6 +69,7 @@ def tile_picked_route2_mlprelu_p_kernel(tc, x_words, x_scales, gate, w1, w2_word
         nc.vector.memset(zero[:], 0.0)
         nc.vector.memset(xs_win[:].bitcast(I32), 0)
         nc.vector.memset(w2_sc[:].bitcast(I32), 0)
+        nc.vector.memset(xs_last[:].bitcast(I32), 0)
         nc.scalar.activation(out=placed[0][:], in_=zero[:].to_broadcast([P, U]), func=RELU)
 
         def load_w1(g):
@@ -78,17 +79,12 @@ def tile_picked_route2_mlprelu_p_kernel(tc, x_words, x_scales, gate, w1, w2_word
         def load_x(g):
             nc.sync.dma_start(out=x_win[g][:], in_=x_words[g].rearrange("p n t -> p (n t)").bitcast(I32))
 
-        for q in range(2):
+        for q in (0, 2, 1, 3):
             nc.sync.dma_start(
-                out=xs_rows[32 * q : 32 * q + 4 * PASSES, :],
-                in_=x_scales[:, 4 * q : 4 * q + 4, :].bitcast(I32),
+                out=xs_rows[32 * q : 32 * q + 4, :],
+                in_=x_scales[0, 4 * q : 4 * q + 4, :].bitcast(I32),
             )
-        for q in range(2, 4):
-            for g in range(PASSES):
-                nc.sync.dma_start(
-                    out=xs_rows[32 * q + 4 * g : 32 * q + 4 * g + 4, :],
-                    in_=x_scales[g, 4 * q : 4 * q + 4, :].bitcast(I32),
-                )
+        nc.sync.dma_start(out=xs_rows[4:20, :], in_=x_scales[1].bitcast(I32))
         nc.sync.dma_start(offs_sb[:], offs)
         load_w1(0)
         load_x(0)
@@ -99,10 +95,7 @@ def tile_picked_route2_mlprelu_p_kernel(tc, x_words, x_scales, gate, w1, w2_word
                 in_=w2_scales[0, 4 * q : 4 * q + 4, :].bitcast(I32),
             )
         load_x(1)
-        nc.sync.dma_start(out=w2_codes[:], in_=w2_words[0].rearrange("p n t -> p (n t)").bitcast(I32))
-        nc.sync.dma_start(out=gate_sb[:, :CHUNK], in_=gate[:, :CHUNK])
         nc.sync.dma_start(dst_sb[:], dst)
-        nc.sync.dma_start(out=gate_sb[:, CHUNK:], in_=gate[:, CHUNK:])
 
         def entries(tile, a, b):
             return tile[:, a // LANES : b // LANES]
@@ -140,7 +133,7 @@ def tile_picked_route2_mlprelu_p_kernel(tc, x_words, x_scales, gate, w1, w2_word
                     lhsT=w1_codes[g][:, chans].bitcast(FP8X4),
                     lhsT_scale=w1_sc[g][:, chans],
                     rhs=picked(g, i * TILE, (i + 1) * TILE).bitcast(FP8X4),
-                    rhs_scale=xs_pick[4 * g :, cols],
+                    rhs_scale=(xs_pick, xs_last)[g][:, cols],
                     start=(g == 0 and t == 0),
                     stop=(g == PASSES - 1 and t == PACK - 1),
                 )
@@ -186,9 +179,18 @@ def tile_picked_route2_mlprelu_p_kernel(tc, x_words, x_scales, gate, w1, w2_word
             nc.scalar.activation(out=placed[1][:].indirect(entries(dst_sb, a, e)), in_=y_gated[:, a:e], func=COPY)
 
         for q in range(4):
-            live = slice(32 * q, 32 * q + 4 * PASSES)
+            live = slice(32 * q, 32 * q + (20 if q == 0 else 4))
             nc.vector.tensor_copy(out=xs_win[live, :].bitcast(I32), in_=xs_rows[live, :])
         nc.vector.tensor_copy(out=xs_pick[:], in_=xs_win[:].indirect(offs_sb[:]))
+        for q in (0, 2, 1, 3):
+            nc.sync.dma_start(
+                out=xs_last[32 * q : 32 * q + 4, :].bitcast(I32), in_=xs_pick[4 + 4 * q : 8 + 4 * q, :].bitcast(I32)
+            )
+        w2_codes = shared.tile([P, N], I32, name="w2_codes", align_bytes=64, offset=0)
+        gate_sb = shared.tile([P, S], F32, name="gate_sb", align_bytes=64, offset=4 * N)
+        nc.sync.dma_start(out=w2_codes[:], in_=w2_words[0].rearrange("p n t -> p (n t)").bitcast(I32))
+        nc.sync.dma_start(out=gate_sb[:, :CHUNK], in_=gate[:, :CHUNK])
+        nc.sync.dma_start(out=gate_sb[:, CHUNK:], in_=gate[:, CHUNK:])
         weave(0, 0, SHARE[0], nc.vector.tensor_copy)
         weave(0, SHARE[0], P, nc.scalar.copy)
         placed.append(keep.tile([P, U], F32, name="placed1", tag="stage0", align_bytes=64))

from contextlib import ExitStack

import concourse.mybir as mybir

K, T, S, H, N, U = 1024, 2048, 1024, 512, 256, 2048
FLOPS = 2 * K * H * S + 2 * H * N * S

F32 = mybir.dt.float32
BF16 = mybir.dt.bfloat16
I32 = mybir.dt.int32
U32 = mybir.dt.uint32
U16 = mybir.dt.uint16
U8 = mybir.dt.uint8
FP8X4 = mybir.dt.float8_e4m3fn_x4
RELU = mybir.ActivationFunctionType.Relu
COPY = mybir.ActivationFunctionType.Copy
MULT = mybir.AluOpType.mult

P = 128
PACK = 4
PASSES = K // (P * PACK)
TILE = 128
CHUNK = 256
LANES = 16
SHARE = (48, 64)
H_PIECES = ((0, 128), (128, 256), (256, 512), (512, 768), (768, 1024))
HELD = 256
H_BANK = (0, 1, 2, 3, 4, 5, 7, 6)


def tile_picked_route2_mlprelu_p_kernel(tc, x_words, x_scales, gate, w1, w2_words, w2_scales, offs, dst, out):
    nc = tc.nc
    with ExitStack() as ctx:
        keep = ctx.enter_context(tc.tile_pool(name="keep", bufs=1))
        shared = ctx.enter_context(tc.tile_pool(name="shared", bufs=1))
        psum = ctx.enter_context(tc.psum_pool(name="psum", bufs=1))

        offs_sb = keep.tile([P, S // LANES], U16, name="offs_sb")
        dst_sb = keep.tile([P, S // LANES], U16, name="dst_sb")
        x_win = [keep.tile([P, T], I32, name="x_win%d" % g, align_bytes=64) for g in range(PASSES)]
        xs_rows = keep.tile([P, T // 4], I32, name="xs_rows", align_bytes=64)
        xs_win = shared.tile([P, T], U8, name="xs_win", align_bytes=64, offset=0)
        x_pick = [keep.tile([P, S - g * HELD], U32, name="x_pick%d" % g, align_bytes=64) for g in range(PASSES)]
        xs_pick = keep.tile([P, S], U8, name="xs_pick", align_bytes=64)
        w1_raw = [
            keep.tile([P, PACK * H], F32, name="w1_raw%d" % g, tag="stage%d" % g, align_bytes=64)
            for g in range(PASSES)
        ]
        w1_bf = [keep.tile([P, PACK * H], BF16, name="w1_bf%d" % g, align_bytes=64) for g in range(PASSES)]
        w1_codes = [keep.tile([P, H], U32, name="w1_codes%d" % g, align_bytes=64) for g in range(PASSES)]
        w1_sc = [keep.tile([P, H], U8, name="w1_sc%d" % g, align_bytes=64) for g in range(PASSES)]
        xs_last = keep.tile([P, S], U8, name="xs_last", align_bytes=64)
        w2_sc = keep.tile([P, N], U8, name="w2_sc", align_bytes=64)
        h_bf = [
            keep.tile([P, PACK * (b - a)], BF16, name="h_bf%d" % a, tag="h_bf%d" % a, align_bytes=64)
            for a, b in H_PIECES[:3]
        ]
        h_codes = [
            keep.tile([P, CHUNK], U32, name="h_codes%d" % c, tag="h_codes%d" % c, align_bytes=64)
            for c in range(S // CHUNK)
        ]
        h_sc = [keep.tile([P, CHUNK], U8, name="h_sc0", tag="h_sc01", align_bytes=64)]
        y_plain = keep.tile([P, S], F32, name="y_plain", align_bytes=64)
        y_gated = keep.tile([P, S], F32, name="y_gated", align_bytes=64)
        placed = [keep.tile([P, U], F32, name="placed0", align_bytes=64)]
        zero = keep.tile([P, 1], F32, name="zero", align_bytes=64)
        banks = [psum.tile([P, PACK * TILE], F32, name="bank%d" % i) for i in range(S // TILE)]

        nc.vector.memset(zero[:], 0.0)
        nc.vector.memset(xs_win[:].bitcast(I32), 0)
        nc.vector.memset(w2_sc[:].bitcast(I32), 0)
        nc.vector.memset(xs_last[:].bitcast(I32), 0)
        nc.scalar.activation(out=placed[0][:], in_=zero[:].to_broadcast([P, U]), func=RELU)

        def load_w1(g):
            rows = w1[g * P * PACK : (g + 1) * P * PACK, :]
            nc.sync.dma_start(out=w1_raw[g][:], in_=rows.rearrange("(p j) c -> p (j c)", j=PACK))

        def load_x(g):
            nc.sync.dma_start(out=x_win[g][:], in_=x_words[g].rearrange("p n t -> p (n t)").bitcast(I32))

        for q in (0, 2, 1, 3):
            nc.sync.dma_start(
                out=xs_rows[32 * q : 32 * q + 4, :],
                in_=x_scales[0, 4 * q : 4 * q + 4, :].bitcast(I32),
            )
        nc.sync.dma_start(out=xs_rows[4:20, :], in_=x_scales[1].bitcast(I32))
        nc.sync.dma_start(offs_sb[:], offs)
        load_w1(0)
        load_x(0)
        load_w1(1)
        for q in range(4):
            nc.sync.dma_start(
                out=w2_sc[32 * q : 32 * q + 4, :].bitcast(I32),
                in_=w2_scales[0, 4 * q : 4 * q + 4, :].bitcast(I32),
            )
        load_x(1)
        nc.sync.dma_start(dst_sb[:], dst)

        def entries(tile, a, b):
            return tile[:, a // LANES : b // LANES]

        def picked(g, a, b):
            if g == 1 and a >= S - HELD:
                return x_pick[2][:, a - S + HELD : b - S + HELD]
            return x_pick[g][:, a:b]

        def h_values(a, b):
            n = [lo <= a < hi for lo, hi in H_PIECES].index(True)
            lo = H_PIECES[n][0]
            return h_bf[n][:, PACK * (a - lo) : PACK * (b - lo)]

        def gather_words(g, a, b):
            nc.vector.tensor_copy(
                out=picked(g, a, b), in_=x_win[g][:].bitcast(U32).indirect(entries(offs_sb, a, b))
            )

        def weave(g, a, b, copy):
            copy(
                out=w1_bf[g][:].rearrange("p (t m j) -> p m j t", t=PACK, j=PACK)[:, a:b],
                in_=w1_raw[g][:].rearrange("p (j m t) -> p m j t", j=PACK, t=PACK)[:, a:b],
            )

        def quantize_w1(g):
            nc.vector.quantize_mx(out=w1_codes[g][:].bitcast(FP8X4), scales=w1_sc[g][:], in_=w1_bf[g][:])

        def h_passes(i, g):
            cols = slice(i * TILE, (i + 1) * TILE)
            for t in range(PACK):
                chans = slice(t * P, (t + 1) * P)
                nc.tensor.matmul_mx(
                    out=banks[H_BANK[i]][:, t * TILE : (t + 1) * TILE],
                    lhsT=w1_codes[g][:, chans].bitcast(FP8X4),
                    lhsT_scale=w1_sc[g][:, chans],
                    rhs=picked(g, i * TILE, (i + 1) * TILE).bitcast(FP8X4),
                    rhs_scale=(xs_pick, xs_last)[g][:, cols],
                    start=(g == 0 and t == 0),
                    stop=(g == PASSES - 1 and t == PACK - 1),
                )

        def relu(i):
            nc.scalar.activation(
                out=h_values(i * TILE, (i + 1) * TILE).rearrange("p (c i t) -> p c t i", i=2, t=PACK),
                in_=banks[H_BANK[i]][:].rearrange("p (t c i) -> p c t i", i=2, t=PACK),
                func=RELU,
            )

        def quantize_h(a, b):
            nc.vector.quantize_mx(
                out=h_codes[a // CHUNK][:, a % CHUNK : a % CHUNK + b - a].bitcast(FP8X4), scales=h_sc[a // CHUNK][:, a % CHUNK : a % CHUNK + b - a], in_=h_values(a, b)
            )

        def y_pass(b, c, bank, at=0):
            rows = slice(b * P, (b + 1) * P)
            nc.tensor.matmul_mx(
                out=banks[bank][:, at : at + CHUNK],
                lhsT=w2_codes[:, rows].bitcast(FP8X4),
                lhsT_scale=w2_sc[:, rows],
                rhs=h_codes[c][:].bitcast(FP8X4),
                rhs_scale=h_sc[c][:],
                start=True,
                stop=True,
            )

        def copy_y0(c, bank):
            nc.scalar.copy(out=y_plain[:, c * CHUNK : (c + 1) * CHUNK], in_=banks[bank][:, :CHUNK])

        def gate_y1(c, bank, at=0):
            cols = slice(c * CHUNK, (c + 1) * CHUNK)
            nc.vector.tensor_tensor(y_gated[:, cols], banks[bank][:, at : at + CHUNK], gate_sb[:, cols], MULT)

        def scatter0(c):
            a, e = c * CHUNK, (c + 1) * CHUNK
            nc.vector.tensor_tensor(
                placed[0][:].indirect(entries(dst_sb, a, e)), y_plain[:, a:e], gate_sb[:, a:e], MULT
            )

        def scatter1(a, e):
            nc.scalar.activation(out=placed[1][:].indirect(entries(dst_sb, a, e)), in_=y_gated[:, a:e], func=COPY)

        for q in range(4):
            live = slice(32 * q, 32 * q + (20 if q == 0 else 4))
            nc.vector.tensor_copy(out=xs_win[live, :].bitcast(I32), in_=xs_rows[live, :])
        nc.vector.tensor_copy(out=xs_pick[:], in_=xs_win[:].indirect(offs_sb[:]))
        for q in (0, 2, 1, 3):
            nc.sync.dma_start(
                out=xs_last[32 * q : 32 * q + 4, :].bitcast(I32), in_=xs_pick[4 + 4 * q : 8 + 4 * q, :].bitcast(I32)
            )
        w2_codes = shared.tile([P, N], I32, name="w2_codes", align_bytes=64, offset=0)
        gate_sb = shared.tile([P, S], F32, name="gate_sb", align_bytes=64, offset=4 * N)
        nc.sync.dma_start(out=w2_codes[:], in_=w2_words[0].rearrange("p n t -> p (n t)").bitcast(I32))
        nc.sync.dma_start(out=gate_sb[:, :CHUNK], in_=gate[:, :CHUNK])
        nc.sync.dma_start(out=gate_sb[:, CHUNK:], in_=gate[:, CHUNK:])
        weave(0, 0, SHARE[0], nc.vector.tensor_copy)
        weave(0, SHARE[0], P, nc.scalar.copy)
        placed.append(keep.tile([P, U], F32, name="placed1", tag="stage0", align_bytes=64))
        nc.scalar.activation(out=placed[1][:], in_=zero[:].to_broadcast([P, U]), func=RELU)
        quantize_w1(0)
        for a, b in ((0, TILE), (TILE, 3 * TILE), (3 * TILE, 3 * CHUNK), (3 * CHUNK, S)):
            gather_words(0, a, b)
        for i in range(S // TILE):
            h_passes(i, 0)
        weave(1, 0, SHARE[1], nc.vector.tensor_copy)
        weave(1, SHARE[1], P, nc.scalar.copy)
        quantize_w1(1)
        for a, b in ((0, TILE), (TILE, CHUNK), (CHUNK, 2 * CHUNK), (2 * CHUNK, S - HELD)):
            gather_words(1, a, b)
            for i in range(a // TILE, b // TILE):
                h_passes(i, 1)

        for i in range(2):
            relu(i)
            quantize_h(i * TILE, (i + 1) * TILE)
        x_pick.append(keep.tile([P, HELD], U32, name="x_pick_last", tag="h_bf128", align_bytes=64))
        gather_words(1, S - HELD, S)
        relu(2)
        relu(3)
        y_pass(0, 0, 0)
        copy_y0(0, 0)
        y_pass(1, 0, 1)
        gate_y1(0, 1)
        h_sc.append(keep.tile([P, CHUNK], U8, name="h_sc1", tag="h_sc01", align_bytes=64))
        h_sc.extend(keep.tile([P, CHUNK], U8, name="h_sc%d" % c, align_bytes=64) for c in (2, 3))
        quantize_h(CHUNK, 2 * CHUNK)
        scatter0(0)
        h_bf.append(keep.tile([P, PACK * CHUNK], BF16, name="h_bf512", tag="h_codes0", align_bytes=64))
        relu(4)
        relu(5)
        quantize_h(2 * CHUNK, 3 * CHUNK)
        y_pass(0, 1, 4)
        y_pass(1, 1, 4, CHUNK)
        for i in range((S - HELD) // TILE, S // TILE):
            h_passes(i, 1)
        copy_y0(1, 4)
        gate_y1(1, 4, CHUNK)
        scatter0(1)
        h_bf.append(keep.tile([P, PACK * CHUNK], BF16, name="h_bf768", tag="h_codes1", align_bytes=64))
        relu(6)
        relu(7)
        quantize_h(3 * CHUNK, S)
        y_pass(0, 2, 0)
        copy_y0(2, 0)
        y_pass(1, 2, 6)
        gate_y1(2, 6)
        scatter0(2)
        scatter1(0, 3 * TILE)
        y_pass(0, 3, 7)
        copy_y0(3, 7)
        y_pass(1, 3, 1)
        gate_y1(3, 1)
        scatter0(3)
        nc.sync.dma_start(out=out[0:P, :], in_=placed[0][:])
        scatter1(3 * TILE, 6 * TILE)
        scatter1(6 * TILE, S)
        nc.scalar.dma_start(out=out[P : 2 * P, :], in_=placed[1][:])
